import numpy as np
import ml_dtypes


def mxq(x, axis, fmt="e4m3"):
    dtype, down = {"e4m3": (ml_dtypes.float8_e4m3fn, 7), "e5m2": (ml_dtypes.float8_e5m2, 14)}[fmt]
    v = np.moveaxis(np.asarray(x, np.float32).astype(ml_dtypes.bfloat16).astype(np.float64), axis, -1)
    blocks = v.reshape(v.shape[:-1] + (-1, 32))
    amax = np.abs(blocks).max(-1, keepdims=True)
    byte = np.maximum(np.where(amax > 0, np.frexp(amax)[1] - 1 + 127, 0) - down, 1)
    scale = np.exp2(byte - 127.0)
    codes = (blocks / scale).astype(np.float32).astype(dtype).astype(np.float64)
    return np.moveaxis((codes * scale).reshape(v.shape), -1, axis)


WIDE = False


def mx_kscale(k):
    if not WIDE:
        return np.ones(k)
    levels = np.array([10, -10, 5, -5, 0])
    if k % 512:
        return np.exp2(np.random.permutation(np.resize(levels, k // 32))).repeat(32)
    a = np.empty((k // 512, 16))
    for p in range(k // 512):
        a[p, :8] = np.random.permutation(np.resize(levels, 8))
        for g in range(8):
            far = levels[np.abs(levels - a[p, g]) >= 10]
            a[p, g + 8] = far[np.random.randint(len(far))]
    return np.exp2(a.ravel()).repeat(32)


def f64(x):
    return np.asarray(x).astype(np.float64)


def striped(idx):
    return np.tile(idx.reshape(-1, 16).T, (8, 1)).astype(np.uint16)


def unstriped(offs):
    return offs[:16].T.reshape(-1).astype(np.int64)


def striped8(idx):
    return np.concatenate([x.reshape(-1, 16).T for x in idx]).astype(np.uint16)


def runs(offs, k):
    lists = np.stack([offs[16 * r : 16 * r + 16].T.reshape(-1) for r in range(8)]).astype(np.int64)
    return lists[np.arange(k) % 512 // 64]


def pack_weight(w):
    k, n = w.shape
    w = f64(np.asarray(w, np.float32).astype(ml_dtypes.bfloat16)).reshape(k // 32, 32, n)
    amax = np.abs(w).max(1)
    byte = np.clip(np.where(amax > 0, np.frexp(amax)[1] - 1 + 127 - 7, 1), 1, 254)
    scaled = (w * np.exp2(127.0 - byte)[:, None, :]).reshape(k, n).astype(np.float32)
    words = np.ascontiguousarray(scaled.reshape(k // 512, 128, 4, n).transpose(0, 1, 3, 2)).astype(ml_dtypes.float8_e4m3fn).view(np.uint8)
    return words, np.ascontiguousarray(byte.astype(np.uint8).reshape(k // 512, 16, n))


def unpack_weight(words, scales):
    g, p, n, _ = words.shape
    vals = np.ascontiguousarray(words).view(ml_dtypes.float8_e4m3fn).astype(np.float64) * np.repeat(np.exp2(scales.astype(np.float64) - 127.0), 8, axis=1)[..., None]
    return vals.transpose(0, 1, 3, 2).reshape(g * 512, n)


K, T, S, H = 512, 2048, 512, 512


def setup_inputs():
    n = np.random.standard_normal
    s = mx_kscale(K)[:, None]
    u = mx_kscale(H)
    packed_xT = pack_weight(n((K, T)) * s)
    return {
        "x_words": packed_xT[0],
        "x_scales": packed_xT[1],
        "w1": (n((K, H)) / np.sqrt(K) / s).astype(np.float32),
        "gn": (np.random.uniform(0.5, 1.5, (H, 1)) * u[:, None]).astype(np.float32),
        "w2": (n((H, H)) / np.sqrt(H) / u[:, None]).astype(np.float32),
        "offs": striped(np.random.permutation(T)[:S]),
        "nb": striped8(np.stack([np.random.permutation(S) for _ in range(8)])),
    }


def reference(x_words, x_scales, w1, gn, w2, offs, nb):
    xq = unpack_weight(x_words, x_scales)[:, unstriped(offs)]
    y = mxq(f64(w1), 0, "e4m3").T @ xq
    z = f64(gn) * np.tanh(y)
    w2q = mxq(f64(w2), 0, "e4m3")
    h = np.tanh(y + 0.5 * ((w2q.T @ mxq(z, 0, "e4m3"))))
    z2 = f64(gn) * (h[np.arange(H)[:, None], runs(nb, H)])
    return np.tanh(y + 0.5 * ((w2q.T @ mxq(z2, 0, "e4m3"))))

@@ -1,0 +1,238 @@
+from contextlib import ExitStack
+
+import concourse.mybir as mybir
+
+K, T, S, H = 512, 2048, 512, 512
+FLOPS = 3 * 2 * 512 * 512 * 512
+
+F32 = mybir.dt.float32
+BF16 = mybir.dt.bfloat16
+I32 = mybir.dt.int32
+U32 = mybir.dt.uint32
+U16 = mybir.dt.uint16
+U8 = mybir.dt.uint8
+FP8X4 = mybir.dt.float8_e4m3fn_x4
+ACT = mybir.ActivationFunctionType
+ALU = mybir.AluOpType
+
+P = 128
+PACK = 4
+CHUNK = 128
+CHUNKS = S // CHUNK
+HALF = S // 2
+LIST_COLS = CHUNK // 16
+V_PLANE = 3
+FIRST_REDONE = 2
+
+
+def tile_picked_implicit2_none_p_kernel(
+    tc, x_words, x_scales, w1, gn, w2, offs, nb, out
+):
+    nc = tc.nc
+    with ExitStack() as ctx:
+        keep = ctx.enter_context(tc.tile_pool(name="keep", bufs=1))
+        psum = ctx.enter_context(tc.psum_pool(name="psum", bufs=1))
+
+        def sb(name, shape, dtype):
+            return keep.tile(shape, dtype, name=name, align_bytes=64)
+
+        def cols(i, width):
+            return slice(i * width, (i + 1) * width)
+
+        def mx(dst, w_codes, w_scales, t, a_codes, a_scales, span, start, stop):
+            nc.tensor.matmul_mx(
+                out=dst,
+                lhsT=w_codes[:, cols(t, P)].bitcast(FP8X4),
+                lhsT_scale=w_scales[:, cols(t, P)],
+                rhs=a_codes[:, span].bitcast(FP8X4),
+                rhs_scale=a_scales[:, span],
+                start=start,
+                stop=stop,
+            )
+
+        offs_t = keep.tile([P, S // 16], U16, name="offs_t")
+        nb_t = keep.tile([P, S // 16], U16, name="nb_t")
+        w1_raw = [sb("w1_raw%d" % u, [P, PACK, H // 2], F32) for u in range(2)]
+        w2_raw = [sb("w2_raw%d" % u, [P, PACK, H // 2], F32) for u in range(2)]
+        xw = sb("xw", [P, T], U32)
+        xs = sb("xs", [P, T], U8)
+        gain = sb("gain", [P, PACK], F32)
+        warm = sb("warm", [P, 2], F32)
+
+        nc.vector.memset(xs[:].bitcast(I32), 0)
+        nc.vector.memset(warm[:, 0:1], 0.0)
+        nc.sync.dma_start(offs_t[:], offs)
+        nc.scalar.dma_start(out=gain[:], in_=gn.rearrange("(p t) o -> p (t o)", t=PACK))
+        w1_rows = w1.rearrange("(p j) c -> p j c", j=PACK)
+        nc.sync.dma_start(out=w1_raw[0][:], in_=w1_rows[:, :, cols(0, H // 2)])
+        for q in range(4):
+            nc.sync.dma_start(
+                out=xs[32 * q : 32 * q + 4, :].bitcast(I32),
+                in_=x_scales[0, 4 * q : 4 * q + 4, :].bitcast(I32),
+            )
+        nc.sync.dma_start(out=w1_raw[1][:], in_=w1_rows[:, :, cols(1, H // 2)])
+        nc.sync.dma_start(
+            out=xw[:].bitcast(I32), in_=x_words[0].rearrange("p n r -> p (n r)").bitcast(I32)
+        )
+        w2_rows = w2.rearrange("(p j) c -> p j c", j=PACK)
+        for u in range(2):
+            nc.sync.dma_start(out=w2_raw[u][:], in_=w2_rows[:, :, cols(u, H // 2)])
+        nc.sync.dma_start(nb_t[:], nb)
+        nc.scalar.activation(warm[:, 1:2], warm[:, 0:1], ACT.Sigmoid)
+
+        gain_woven = sb("gain_woven", [P, CHUNK, PACK], F32)
+        nc.vector.tensor_scalar(
+            gain_woven[:], gain[:].unsqueeze(1).to_broadcast([P, CHUNK, PACK]), 0.5, None, ALU.mult
+        )
+        gain_row = sb("gain_row", [P, CHUNK], F32)
+        nc.vector.tensor_scalar(
+            gain_row[:], gain[:, V_PLANE : V_PLANE + 1].to_broadcast([P, CHUNK]), 0.5, None, ALU.mult
+        )
+
+        xq_scales = sb("xq_scales", [P, S], U8)
+        nc.vector.tensor_copy(xq_scales[:], xs[:].indirect(offs_t[:]))
+
+        def weave(copy, grouped, raw, m_dst, m_src):
+            copy(
+                out=grouped[:].rearrange("p t m j -> p m j t")[:, m_dst],
+                in_=raw[:].rearrange("p j (m t) -> p m j t", t=PACK)[:, m_src],
+            )
+
+        def quantize_weight(name, grouped):
+            codes = sb(name + "_codes", [P, H], U32)
+            scales = sb(name + "_scales", [P, H], U8)
+            nc.vector.quantize_mx(
+                out=codes[:].bitcast(FP8X4),
+                scales=scales[:],
+                in_=grouped[:].rearrange("p t m j -> p (t m j)"),
+            )
+            return codes, scales
+
+        w1_grouped = sb("w1_grouped", [P, PACK, P, PACK], BF16)
+        weave(nc.scalar.copy, w1_grouped, w1_raw[0], slice(0, 64), slice(0, 64))
+        weave(nc.vector.tensor_copy, w1_grouped, w1_raw[1], slice(64, P), slice(0, 64))
+        w1_codes, w1_scales = quantize_weight("w1", w1_grouped)
+
+        xq_codes = sb("xq_codes", [P, S], U32)
+        for u in range(2):
+            nc.vector.tensor_copy(
+                xq_codes[:, cols(u, HALF)], xw[:].indirect(offs_t[:, cols(u, HALF // 16)])
+            )
+
+        w2_grouped = sb("w2_grouped", [P, PACK, P, PACK], BF16)
+        weave(nc.vector.tensor_copy, w2_grouped, w2_raw[0], slice(0, 64), slice(0, 64))
+
+        y_sb = sb("y_sb", [P, PACK, S], F32)
+        z_codes = sb("z_codes", [P, S], U32)
+        z_scales = sb("z_scales", [P, S], U8)
+        z_bf = []
+        y_banks = []
+        for c in range(CHUNKS):
+            bank = psum.tile([P, PACK, CHUNK], F32, name="chunk_bank%d" % c)
+            y_banks.append(bank)
+            for t in range(PACK):
+                mx(bank[:, t, :], w1_codes, w1_scales, t, xq_codes, xq_scales, cols(c, CHUNK), True, True)
+            th = sb("th%d" % c, [P, CHUNK, PACK], F32)
+            nc.scalar.activation(th[:], bank[:].rearrange("p t n -> p n t"), ACT.Tanh)
+            zb = sb("z_bf%d" % c, [P, CHUNK * PACK], BF16)
+            nc.vector.tensor_tensor(
+                zb[:],
+                th[:].rearrange("p n t -> p (n t)"),
+                gain_woven[:].rearrange("p n t -> p (n t)"),
+                ALU.mult,
+            )
+            z_bf.append(zb)
+            if c > 0:
+                nc.vector.quantize_mx(
+                    out=z_codes[:, cols(c - 1, CHUNK)].bitcast(FP8X4),
+                    scales=z_scales[:, cols(c - 1, CHUNK)],
+                    in_=z_bf[c - 1][:],
+                )
+        weave(nc.scalar.copy, w2_grouped, w2_raw[1], slice(64, P), slice(0, 64))
+        nc.vector.quantize_mx(
+            out=z_codes[:, cols(CHUNKS - 1, CHUNK)].bitcast(FP8X4),
+            scales=z_scales[:, cols(CHUNKS - 1, CHUNK)],
+            in_=z_bf[CHUNKS - 1][:],
+        )
+        w2_codes = sb("w2_codes", [P, H], U32)
+        w2_scales = sb("w2_scales", [P, H], U8)
+        for t in range(PACK):
+            nc.vector.quantize_mx(
+                out=w2_codes[:, cols(t, P)].bitcast(FP8X4),
+                scales=w2_scales[:, cols(t, P)],
+                in_=w2_grouped[:, t].rearrange("p m j -> p (m j)"),
+            )
+
+        windows = [sb("window%d" % t, [P, S], F32) for t in range(PACK)]
+        for t in range(PACK):
+            bank = psum.tile([P, S], F32, name="plane_bank%d" % t)
+            if t == V_PLANE:
+                mx(bank[:], w1_codes, w1_scales, t, xq_codes, xq_scales, slice(0, S), True, False)
+                mx(bank[:], w2_codes, w2_scales, t, z_codes, z_scales, slice(0, S), False, True)
+                nc.scalar.activation(windows[t][:], bank[:], ACT.Tanh)
+                for c in range(FIRST_REDONE):
+                    nc.scalar.copy(out=y_sb[:, t, cols(c, CHUNK)], in_=y_banks[c][:, t, :])
+            else:
+                for c in range(CHUNKS):
+                    nc.scalar.copy(out=y_sb[:, t, cols(c, CHUNK)], in_=y_banks[c][:, t, :])
+                mx(bank[:], w2_codes, w2_scales, t, z_codes, z_scales, slice(0, S), True, True)
+                nc.vector.tensor_tensor(windows[t][:], bank[:], y_sb[:, t, :], ALU.add)
+
+        z2_codes = sb("z2_codes", [P, S], U32)
+        z2_scales = sb("z2_scales", [P, S], U8)
+        out_rows = out.rearrange("(p t) n -> p t n", t=PACK)
+
+        def fetch(c):
+            picks = nb_t[:, cols(c, LIST_COLS)]
+            sig = sb("sig%d" % c, [P, PACK - 1, CHUNK], F32)
+            z2_planes = sb("z2_planes%d" % c, [P, PACK, CHUNK], F32)
+            for t in range(PACK - 1):
+                nc.scalar.activation(sig[:, t, :], windows[t][:].indirect(picks), ACT.Sigmoid, scale=2.0)
+            nc.vector.tensor_tensor(
+                z2_planes[:, V_PLANE, :], windows[V_PLANE][:].indirect(picks), gain_row[:], ALU.mult
+            )
+            for t in range(PACK - 1):
+                nc.vector.tensor_scalar(
+                    z2_planes[:, t, :], sig[:, t, :], 0.5, gain[:, t : t + 1], ALU.subtract, ALU.mult
+                )
+            zb = sb("z2_bf%d" % c, [P, CHUNK * PACK], BF16)
+            nc.vector.tensor_copy(
+                out=zb[:].rearrange("p (a i t) -> p a t i", i=4, t=PACK),
+                in_=z2_planes[:].rearrange("p t (a i) -> p a t i", i=4),
+            )
+            return zb
+
+        def finish(c, zb):
+            span = cols(c, CHUNK)
+            nc.vector.quantize_mx(
+                out=z2_codes[:, span].bitcast(FP8X4), scales=z2_scales[:, span], in_=zb[:]
+            )
+            res = sb("res%d" % c, [P, PACK, CHUNK], F32)
+            if c == CHUNKS - 1:
+                for t in range(PACK):
+                    bank = psum.tile([P, CHUNK], F32, name="plane_bank%d" % t)
+                    mx(bank[:], w1_codes, w1_scales, t, xq_codes, xq_scales, span, True, False)
+                    mx(bank[:], w2_codes, w2_scales, t, z2_codes, z2_scales, span, False, True)
+                    nc.scalar.activation(res[:, t, :], bank[:], ACT.Tanh)
+                    if t % 2:
+                        nc.sync.dma_start(out=out_rows[:, t - 1 : t + 1, span], in_=res[:, t - 1 : t + 1, :])
+                return
+            bank = psum.tile([P, PACK, CHUNK], F32, name="chunk_bank%d" % c)
+            redone = c >= FIRST_REDONE
+            for t in range(PACK):
+                if redone:
+                    mx(bank[:, t, :], w1_codes, w1_scales, t, xq_codes, xq_scales, span, True, False)
+                mx(bank[:, t, :], w2_codes, w2_scales, t, z2_codes, z2_scales, span, not redone, True)
+            if redone:
+                nc.scalar.activation(res[:], bank[:], ACT.Tanh)
+            else:
+                pre = sb("pre%d" % c, [P, PACK, CHUNK], F32)
+                nc.vector.tensor_tensor(pre[:], bank[:], y_sb[:, :, span], ALU.add)
+                nc.scalar.activation(res[:], pre[:], ACT.Tanh)
+            nc.sync.dma_start(out=out_rows[:, :, span], in_=res[:])
+
+        staged = fetch(0)
+        for c in range(CHUNKS):
+            ahead = fetch(c + 1) if c + 1 < CHUNKS else None
+            finish(c, staged)
+            staged = ahead

@@ -33,8 +33,8 @@ def tile_picked_implicit2_none_p_kernel(
         keep = ctx.enter_context(tc.tile_pool(name="keep", bufs=1))
         psum = ctx.enter_context(tc.psum_pool(name="psum", bufs=1))
 
-        def sb(name, shape, dtype):
-            return keep.tile(shape, dtype, name=name, align_bytes=64)
+        def sb(name, shape, dtype, tag=None):
+            return keep.tile(shape, dtype, name=name, tag=tag or name, align_bytes=64)
 
         def cols(i, width):
             return slice(i * width, (i + 1) * width)
@@ -52,7 +52,7 @@ def tile_picked_implicit2_none_p_kernel(
 
         offs_t = keep.tile([P, S // 16], U16, name="offs_t")
         nb_t = keep.tile([P, S // 16], U16, name="nb_t")
-        w1_raw = [sb("w1_raw%d" % u, [P, PACK, H // 2], F32) for u in range(2)]
+        w1_raw = sb("w1_raw", [P, PACK, H], F32)
         w2_raw = [sb("w2_raw%d" % u, [P, PACK, H // 2], F32) for u in range(2)]
         xw = sb("xw", [P, T], U32)
         xs = sb("xs", [P, T], U8)
@@ -61,32 +61,32 @@ def tile_picked_implicit2_none_p_kernel(
 
         nc.vector.memset(xs[:].bitcast(I32), 0)
         nc.vector.memset(warm[:, 0:1], 0.0)
+        nc.sync.dma_start(out=gain[:], in_=gn.rearrange("(p t) o -> p (t o)", t=PACK))
         nc.sync.dma_start(offs_t[:], offs)
-        nc.scalar.dma_start(out=gain[:], in_=gn.rearrange("(p t) o -> p (t o)", t=PACK))
-        w1_rows = w1.rearrange("(p j) c -> p j c", j=PACK)
-        nc.sync.dma_start(out=w1_raw[0][:], in_=w1_rows[:, :, cols(0, H // 2)])
+        nc.sync.dma_start(out=w1_raw[:], in_=w1.rearrange("(p j) c -> p j c", j=PACK))
+        nc.sync.dma_start(nb_t[:], nb)
         for q in range(4):
             nc.sync.dma_start(
                 out=xs[32 * q : 32 * q + 4, :].bitcast(I32),
                 in_=x_scales[0, 4 * q : 4 * q + 4, :].bitcast(I32),
             )
-        nc.sync.dma_start(out=w1_raw[1][:], in_=w1_rows[:, :, cols(1, H // 2)])
         nc.sync.dma_start(
             out=xw[:].bitcast(I32), in_=x_words[0].rearrange("p n r -> p (n r)").bitcast(I32)
         )
         w2_rows = w2.rearrange("(p j) c -> p j c", j=PACK)
         for u in range(2):
             nc.sync.dma_start(out=w2_raw[u][:], in_=w2_rows[:, :, cols(u, H // 2)])
-        nc.sync.dma_start(nb_t[:], nb)
         nc.scalar.activation(warm[:, 1:2], warm[:, 0:1], ACT.Sigmoid)
 
         gain_woven = sb("gain_woven", [P, CHUNK, PACK], F32)
         nc.vector.tensor_scalar(
             gain_woven[:], gain[:].unsqueeze(1).to_broadcast([P, CHUNK, PACK]), 0.5, None, ALU.mult
         )
-        gain_row = sb("gain_row", [P, CHUNK], F32)
+        neg_half_gain = sb("neg_half_gain", [P, PACK], F32)
+        nc.vector.tensor_scalar(neg_half_gain[:], gain[:], -0.5, None, ALU.mult)
+        gain_row = sb("gain_row", [P, HALF], F32)
         nc.vector.tensor_scalar(
-            gain_row[:], gain[:, V_PLANE : V_PLANE + 1].to_broadcast([P, CHUNK]), 0.5, None, ALU.mult
+            gain_row[:], gain[:, V_PLANE : V_PLANE + 1].to_broadcast([P, HALF]), 0.5, None, ALU.mult
         )
 
         xq_scales = sb("xq_scales", [P, S], U8)
@@ -99,7 +99,7 @@ def tile_picked_implicit2_none_p_kernel(
             )
 
         def quantize_weight(name, grouped):
-            codes = sb(name + "_codes", [P, H], U32)
+            codes = sb(name + "_codes", [P, H], U32, tag="xs")
             scales = sb(name + "_scales", [P, H], U8)
             nc.vector.quantize_mx(
                 out=codes[:].bitcast(FP8X4),
@@ -109,11 +109,11 @@ def tile_picked_implicit2_none_p_kernel(
             return codes, scales
 
         w1_grouped = sb("w1_grouped", [P, PACK, P, PACK], BF16)
-        weave(nc.scalar.copy, w1_grouped, w1_raw[0], slice(0, 64), slice(0, 64))
-        weave(nc.vector.tensor_copy, w1_grouped, w1_raw[1], slice(64, P), slice(0, 64))
+        weave(nc.scalar.copy, w1_grouped, w1_raw, slice(0, 80), slice(0, 80))
+        weave(nc.vector.tensor_copy, w1_grouped, w1_raw, slice(80, P), slice(80, P))
         w1_codes, w1_scales = quantize_weight("w1", w1_grouped)
 
-        xq_codes = sb("xq_codes", [P, S], U32)
+        xq_codes = sb("xq_codes", [P, S], U32, tag="w1_grouped")
         for u in range(2):
             nc.vector.tensor_copy(
                 xq_codes[:, cols(u, HALF)], xw[:].indirect(offs_t[:, cols(u, HALF // 16)])
@@ -182,57 +182,75 @@ def tile_picked_implicit2_none_p_kernel(
         z2_scales = sb("z2_scales", [P, S], U8)
         out_rows = out.rearrange("(p t) n -> p t n", t=PACK)
 
+        spans = [slice(0, HALF), slice(HALF, HALF + CHUNK), slice(HALF + CHUNK, S)]
+
+        def open_redone(c, names):
+            banks = []
+            for t in range(PACK):
+                bank = psum.tile([P, CHUNK], F32, name=names[t])
+                mx(bank[:], w1_codes, w1_scales, t, xq_codes, xq_scales, spans[c], True, False)
+                banks.append(bank)
+            return banks
+
+        def close_redone(c, banks):
+            for t in range(PACK):
+                mx(banks[t][:], w2_codes, w2_scales, t, z2_codes, z2_scales, spans[c], False, True)
+                nc.scalar.activation(res[c][:, t, :], banks[t][:], ACT.Tanh)
+                if t % 2:
+                    nc.sync.dma_start(out=out_rows[:, t - 1 : t + 1, spans[c]], in_=res[c][:, t - 1 : t + 1, :])
+
+        banks_b = open_redone(1, ["plane_bank%d" % t for t in range(PACK)])
+
         def fetch(c):
-            picks = nb_t[:, cols(c, LIST_COLS)]
-            sig = sb("sig%d" % c, [P, PACK - 1, CHUNK], F32)
-            z2_planes = sb("z2_planes%d" % c, [P, PACK, CHUNK], F32)
+            span = spans[c]
+            n = span.stop - span.start
+            picks = nb_t[:, span.start // 16 : span.stop // 16]
+            sig = sb("sig%d" % c, [P, PACK - 1, n], F32)
+            z2_planes = sb("z2_planes%d" % c, [P, PACK, n], F32)
             for t in range(PACK - 1):
                 nc.scalar.activation(sig[:, t, :], windows[t][:].indirect(picks), ACT.Sigmoid, scale=2.0)
             nc.vector.tensor_tensor(
-                z2_planes[:, V_PLANE, :], windows[V_PLANE][:].indirect(picks), gain_row[:], ALU.mult
+                z2_planes[:, V_PLANE, :], windows[V_PLANE][:].indirect(picks), gain_row[:, :n], ALU.mult
             )
+            return sig, z2_planes
+
+        def quantize_z2(c, sig, z2_planes):
+            span = spans[c]
+            n = span.stop - span.start
             for t in range(PACK - 1):
-                nc.vector.tensor_scalar(
-                    z2_planes[:, t, :], sig[:, t, :], 0.5, gain[:, t : t + 1], ALU.subtract, ALU.mult
-                )
-            zb = sb("z2_bf%d" % c, [P, CHUNK * PACK], BF16)
+                if c == 2:
+                    nc.scalar.activation(
+                        z2_planes[:, t, :], sig[:, t, :], ACT.Identity,
+                        bias=neg_half_gain[:, t : t + 1], scale=gain[:, t : t + 1],
+                    )
+                else:
+                    nc.vector.tensor_scalar(
+                        z2_planes[:, t, :], sig[:, t, :], 0.5, gain[:, t : t + 1], ALU.subtract, ALU.mult
+                    )
+            zb = sb("z2_bf%d" % c, [P, n * PACK], BF16)
             nc.vector.tensor_copy(
                 out=zb[:].rearrange("p (a i t) -> p a t i", i=4, t=PACK),
                 in_=z2_planes[:].rearrange("p t (a i) -> p a t i", i=4),
             )
-            return zb
-
-        def finish(c, zb):
-            span = cols(c, CHUNK)
             nc.vector.quantize_mx(
                 out=z2_codes[:, span].bitcast(FP8X4), scales=z2_scales[:, span], in_=zb[:]
             )
-            res = sb("res%d" % c, [P, PACK, CHUNK], F32)
-            if c == CHUNKS - 1:
-                for t in range(PACK):
-                    bank = psum.tile([P, CHUNK], F32, name="plane_bank%d" % t)
-                    mx(bank[:], w1_codes, w1_scales, t, xq_codes, xq_scales, span, True, False)
-                    mx(bank[:], w2_codes, w2_scales, t, z2_codes, z2_scales, span, False, True)
-                    nc.scalar.activation(res[:, t, :], bank[:], ACT.Tanh)
-                    if t % 2:
-                        nc.sync.dma_start(out=out_rows[:, t - 1 : t + 1, span], in_=res[:, t - 1 : t + 1, :])
-                return
-            bank = psum.tile([P, PACK, CHUNK], F32, name="chunk_bank%d" % c)
-            redone = c >= FIRST_REDONE
-            for t in range(PACK):
-                if redone:
-                    mx(bank[:, t, :], w1_codes, w1_scales, t, xq_codes, xq_scales, span, True, False)
-                mx(bank[:, t, :], w2_codes, w2_scales, t, z2_codes, z2_scales, span, not redone, True)
-            if redone:
-                nc.scalar.activation(res[:], bank[:], ACT.Tanh)
-            else:
-                pre = sb("pre%d" % c, [P, PACK, CHUNK], F32)
-                nc.vector.tensor_tensor(pre[:], bank[:], y_sb[:, :, span], ALU.add)
-                nc.scalar.activation(res[:], pre[:], ACT.Tanh)
-            nc.sync.dma_start(out=out_rows[:, :, span], in_=res[:])
 
-        staged = fetch(0)
-        for c in range(CHUNKS):
-            ahead = fetch(c + 1) if c + 1 < CHUNKS else None
-            finish(c, staged)
-            staged = ahead
+        fetched = [fetch(c) for c in range(3)]
+        quantize_z2(0, *fetched[0])
+        res = [sb("res%d" % c, [P, PACK, spans[c].stop - spans[c].start], F32) for c in range(3)]
+        for u in range(2):
+            pair = slice(2 * u, 2 * u + 2)
+            bank = psum.tile([P, 2, HALF], F32, name="chunk_bank%d" % u)
+            for a in range(2):
+                mx(bank[:, a, :], w2_codes, w2_scales, 2 * u + a, z2_codes, z2_scales, spans[0], True, True)
+            pre = sb("pre%d" % u, [P, 2, HALF], F32)
+            nc.vector.tensor_tensor(pre[:], bank[:], y_sb[:, pair, spans[0]], ALU.add)
+            nc.scalar.activation(res[0][:, pair, :], pre[:], ACT.Tanh)
+            nc.sync.dma_start(out=out_rows[:, pair, spans[0]], in_=res[0][:, pair, :])
+
+        banks_c = open_redone(2, ["chunk_bank%d" % b for b in (2, 3, 0, 1)])
+        quantize_z2(1, *fetched[1])
+        close_redone(1, banks_b)
+        quantize_z2(2, *fetched[2])
+        close_redone(2, banks_c)

@@ -20,9 +20,8 @@ PACK = 4
 CHUNK = 128
 CHUNKS = S // CHUNK
 HALF = S // 2
-LIST_COLS = CHUNK // 16
-V_PLANE = 3
-FIRST_REDONE = 2
+W1_SCALAR = 72
+W2_SCALAR = 32
 
 
 def tile_picked_implicit2_none_p_kernel(
@@ -59,59 +58,41 @@ def tile_picked_implicit2_none_p_kernel(
         gain = sb("gain", [P, PACK], F32)
         warm = sb("warm", [P, 2], F32)
 
-        nc.vector.memset(xs[:].bitcast(I32), 0)
+        nc.gpsimd.memset(xs[:].bitcast(I32), 0)
         nc.vector.memset(warm[:, 0:1], 0.0)
-        nc.sync.dma_start(out=gain[:], in_=gn.rearrange("(p t) o -> p (t o)", t=PACK))
+        nc.scalar.dma_start(out=gain[:], in_=gn.rearrange("(p t) o -> p (t o)", t=PACK))
         nc.sync.dma_start(offs_t[:], offs)
         nc.sync.dma_start(out=w1_raw[:], in_=w1.rearrange("(p j) c -> p j c", j=PACK))
-        nc.sync.dma_start(nb_t[:], nb)
-        for q in range(4):
-            nc.sync.dma_start(
-                out=xs[32 * q : 32 * q + 4, :].bitcast(I32),
-                in_=x_scales[0, 4 * q : 4 * q + 4, :].bitcast(I32),
-            )
+        for r in range(4):
+            nc.sync.dma_start(out=xs[r:P:32, :].bitcast(I32), in_=x_scales[0, r:16:4, :].bitcast(I32))
         nc.sync.dma_start(
             out=xw[:].bitcast(I32), in_=x_words[0].rearrange("p n r -> p (n r)").bitcast(I32)
         )
         w2_rows = w2.rearrange("(p j) c -> p j c", j=PACK)
-        for u in range(2):
-            nc.sync.dma_start(out=w2_raw[u][:], in_=w2_rows[:, :, cols(u, H // 2)])
+        nc.sync.dma_start(out=w2_raw[0][:], in_=w2_rows[:, :, cols(0, H // 2)])
+        nc.sync.dma_start(out=w2_raw[1][:], in_=w2_rows[:, :, cols(1, H // 2)])
+        nc.sync.dma_start(nb_t[:], nb)
         nc.scalar.activation(warm[:, 1:2], warm[:, 0:1], ACT.Sigmoid)
-
-        gain_woven = sb("gain_woven", [P, CHUNK, PACK], F32)
-        nc.vector.tensor_scalar(
-            gain_woven[:], gain[:].unsqueeze(1).to_broadcast([P, CHUNK, PACK]), 0.5, None, ALU.mult
-        )
-        neg_half_gain = sb("neg_half_gain", [P, PACK], F32)
-        nc.vector.tensor_scalar(neg_half_gain[:], gain[:], -0.5, None, ALU.mult)
-        gain_row = sb("gain_row", [P, HALF], F32)
-        nc.vector.tensor_scalar(
-            gain_row[:], gain[:, V_PLANE : V_PLANE + 1].to_broadcast([P, HALF]), 0.5, None, ALU.mult
-        )
 
         xq_scales = sb("xq_scales", [P, S], U8)
         nc.vector.tensor_copy(xq_scales[:], xs[:].indirect(offs_t[:]))
 
-        def weave(copy, grouped, raw, m_dst, m_src):
-            copy(
-                out=grouped[:].rearrange("p t m j -> p m j t")[:, m_dst],
-                in_=raw[:].rearrange("p j (m t) -> p m j t", t=PACK)[:, m_src],
+        def weave_views(grouped, raw, m_dst, m_src):
+            return (
+                grouped[:].rearrange("p t m j -> p m j t")[:, m_dst],
+                raw[:].rearrange("p j (m t) -> p m j t", t=PACK)[:, m_src],
             )
-
-        def quantize_weight(name, grouped):
-            codes = sb(name + "_codes", [P, H], U32, tag="xs")
-            scales = sb(name + "_scales", [P, H], U8)
-            nc.vector.quantize_mx(
-                out=codes[:].bitcast(FP8X4),
-                scales=scales[:],
-                in_=grouped[:].rearrange("p t m j -> p (t m j)"),
-            )
-            return codes, scales
 
         w1_grouped = sb("w1_grouped", [P, PACK, P, PACK], BF16)
-        weave(nc.scalar.copy, w1_grouped, w1_raw, slice(0, 80), slice(0, 80))
-        weave(nc.vector.tensor_copy, w1_grouped, w1_raw, slice(80, P), slice(80, P))
-        w1_codes, w1_scales = quantize_weight("w1", w1_grouped)
+        nc.scalar.copy(*weave_views(w1_grouped, w1_raw, slice(0, W1_SCALAR), slice(0, W1_SCALAR)))
+        nc.vector.tensor_copy(*weave_views(w1_grouped, w1_raw, slice(W1_SCALAR, P), slice(W1_SCALAR, P)))
+        w1_codes = sb("w1_codes", [P, H], U32, tag="xs")
+        w1_scales = sb("w1_scales", [P, H], U8)
+        nc.vector.quantize_mx(
+            out=w1_codes[:].bitcast(FP8X4),
+            scales=w1_scales[:],
+            in_=w1_grouped[:].rearrange("p t m j -> p (t m j)"),
+        )
 
         xq_codes = sb("xq_codes", [P, S], U32, tag="w1_grouped")
         for u in range(2):
@@ -120,13 +101,32 @@ def tile_picked_implicit2_none_p_kernel(
             )
 
         w2_grouped = sb("w2_grouped", [P, PACK, P, PACK], BF16)
-        weave(nc.vector.tensor_copy, w2_grouped, w2_raw[0], slice(0, 64), slice(0, 64))
+        nc.vector.tensor_copy(*weave_views(w2_grouped, w2_raw[0], slice(0, P // 2), slice(0, P // 2)))
 
-        y_sb = sb("y_sb", [P, PACK, S], F32)
         z_codes = sb("z_codes", [P, S], U32)
         z_scales = sb("z_scales", [P, S], U8)
-        z_bf = []
+        z_bf = sb("z_bf", [P, S * PACK], BF16)
+        w2_codes = sb("w2_codes", [P, H], U32)
+        w2_scales = sb("w2_scales", [P, H], U8)
+        halves = [cols(u, HALF) for u in range(2)]
+        spans = [halves[0], cols(2, CHUNK), cols(3, CHUNK)]
+
+        def quantize_z(span):
+            nc.vector.quantize_mx(
+                out=z_codes[:, span].bitcast(FP8X4),
+                scales=z_scales[:, span],
+                in_=z_bf[:, span.start * PACK : span.stop * PACK],
+            )
+
+        def quantize_w2(u):
+            nc.vector.quantize_mx(
+                out=w2_codes[:, cols(u, 2 * P)].bitcast(FP8X4),
+                scales=w2_scales[:, cols(u, 2 * P)],
+                in_=w2_grouped[:, 2 * u : 2 * u + 2].rearrange("p t m j -> p (t m j)"),
+            )
+
         y_banks = []
+        tanh_y = []
         for c in range(CHUNKS):
             bank = psum.tile([P, PACK, CHUNK], F32, name="chunk_bank%d" % c)
             y_banks.append(bank)
@@ -134,123 +134,152 @@ def tile_picked_implicit2_none_p_kernel(
                 mx(bank[:, t, :], w1_codes, w1_scales, t, xq_codes, xq_scales, cols(c, CHUNK), True, True)
             th = sb("th%d" % c, [P, CHUNK, PACK], F32)
             nc.scalar.activation(th[:], bank[:].rearrange("p t n -> p n t"), ACT.Tanh)
-            zb = sb("z_bf%d" % c, [P, CHUNK * PACK], BF16)
-            nc.vector.tensor_tensor(
-                zb[:],
-                th[:].rearrange("p n t -> p (n t)"),
-                gain_woven[:].rearrange("p n t -> p (n t)"),
+            tanh_y.append(th)
+        nc.scalar.copy(
+            *weave_views(w2_grouped, w2_raw[1], slice(P - W2_SCALAR, P), slice(P // 2 - W2_SCALAR, P // 2))
+        )
+
+        def make_z(c):
+            nc.vector.scalar_tensor_tensor(
+                z_bf[:, cols(c, CHUNK * PACK)].rearrange("p (n t) -> p n t", t=PACK),
+                tanh_y[c][:],
+                0.5,
+                gain[:].unsqueeze(1).to_broadcast([P, CHUNK, PACK]),
+                ALU.mult,
                 ALU.mult,
             )
-            z_bf.append(zb)
-            if c > 0:
-                nc.vector.quantize_mx(
-                    out=z_codes[:, cols(c - 1, CHUNK)].bitcast(FP8X4),
-                    scales=z_scales[:, cols(c - 1, CHUNK)],
-                    in_=z_bf[c - 1][:],
-                )
-        weave(nc.scalar.copy, w2_grouped, w2_raw[1], slice(64, P), slice(0, 64))
-        nc.vector.quantize_mx(
-            out=z_codes[:, cols(CHUNKS - 1, CHUNK)].bitcast(FP8X4),
-            scales=z_scales[:, cols(CHUNKS - 1, CHUNK)],
-            in_=z_bf[CHUNKS - 1][:],
+
+        make_z(0)
+        make_z(1)
+        make_z(2)
+        nc.vector.tensor_copy(
+            *weave_views(w2_grouped, w2_raw[1], slice(P // 2, P - W2_SCALAR), slice(0, P // 2 - W2_SCALAR))
         )
-        w2_codes = sb("w2_codes", [P, H], U32)
-        w2_scales = sb("w2_scales", [P, H], U8)
-        for t in range(PACK):
-            nc.vector.quantize_mx(
-                out=w2_codes[:, cols(t, P)].bitcast(FP8X4),
-                scales=w2_scales[:, cols(t, P)],
-                in_=w2_grouped[:, t].rearrange("p m j -> p (m j)"),
-            )
+        quantize_z(spans[0])
+        quantize_w2(0)
+        make_z(3)
+        quantize_z(spans[1])
+        y_and_sig = sb("y_and_sig", [P, 6, S], F32, tag="th0")
+        y_sb = y_and_sig[:, 0:PACK, :]
+        y_last = sb("y_last", [P, HALF], F32, tag="th1")
+        for c in range(2):
+            nc.scalar.copy(out=y_sb[:, 1:3, cols(c, CHUNK)], in_=y_banks[c][:, 1:3, :])
+        for c in range(2, CHUNKS):
+            nc.scalar.copy(out=y_sb[:, :, cols(c, CHUNK)], in_=y_banks[c][:])
+        for c in range(2):
+            nc.scalar.copy(out=y_last[:, cols(c, CHUNK)], in_=y_banks[c][:, 3, :])
+        quantize_z(spans[2])
+        quantize_w2(1)
 
         windows = [sb("window%d" % t, [P, S], F32) for t in range(PACK)]
-        for t in range(PACK):
-            bank = psum.tile([P, S], F32, name="plane_bank%d" % t)
-            if t == V_PLANE:
-                mx(bank[:], w1_codes, w1_scales, t, xq_codes, xq_scales, slice(0, S), True, False)
-                mx(bank[:], w2_codes, w2_scales, t, z_codes, z_scales, slice(0, S), False, True)
-                nc.scalar.activation(windows[t][:], bank[:], ACT.Tanh)
-                for c in range(FIRST_REDONE):
-                    nc.scalar.copy(out=y_sb[:, t, cols(c, CHUNK)], in_=y_banks[c][:, t, :])
-            else:
-                for c in range(CHUNKS):
-                    nc.scalar.copy(out=y_sb[:, t, cols(c, CHUNK)], in_=y_banks[c][:, t, :])
-                mx(bank[:], w2_codes, w2_scales, t, z_codes, z_scales, slice(0, S), True, True)
-                nc.vector.tensor_tensor(windows[t][:], bank[:], y_sb[:, t, :], ALU.add)
+        h_banks = [psum.tile([P, S], F32, name="plane_bank%d" % t) for t in range(PACK)]
+        for span in spans:
+            mx(h_banks[0][:, span], w1_codes, w1_scales, 0, xq_codes, xq_scales, span, True, False)
+            mx(h_banks[1][:, span], w2_codes, w2_scales, 1, z_codes, z_scales, span, True, True)
+            mx(h_banks[0][:, span], w2_codes, w2_scales, 0, z_codes, z_scales, span, False, True)
+        nc.scalar.activation(windows[0][:], h_banks[0][:], ACT.Tanh)
+        for t in range(2, PACK):
+            mx(h_banks[t][:], w2_codes, w2_scales, t, z_codes, z_scales, slice(0, S), True, True)
+        for t in range(1, 3):
+            nc.vector.tensor_tensor(windows[t][:], h_banks[t][:], y_sb[:, t, :], ALU.add)
+        nc.vector.tensor_tensor(windows[3][:, halves[1]], h_banks[3][:, halves[1]], y_sb[:, 3, halves[1]], ALU.add)
+        nc.vector.tensor_tensor(windows[3][:, halves[0]], h_banks[3][:, halves[0]], y_last[:], ALU.add)
+
+        gain_row = sb("gain_row", [P, HALF], F32)
+        nc.scalar.activation(gain_row[:], gain[:, 0:1].to_broadcast([P, HALF]), ACT.Copy, scale=0.5)
 
         z2_codes = sb("z2_codes", [P, S], U32)
         z2_scales = sb("z2_scales", [P, S], U8)
         out_rows = out.rearrange("(p t) n -> p t n", t=PACK)
-
-        spans = [slice(0, HALF), slice(HALF, HALF + CHUNK), slice(HALF + CHUNK, S)]
-
-        def open_redone(c, names):
-            banks = []
-            for t in range(PACK):
-                bank = psum.tile([P, CHUNK], F32, name=names[t])
-                mx(bank[:], w1_codes, w1_scales, t, xq_codes, xq_scales, spans[c], True, False)
-                banks.append(bank)
-            return banks
-
-        def close_redone(c, banks):
-            for t in range(PACK):
-                mx(banks[t][:], w2_codes, w2_scales, t, z2_codes, z2_scales, spans[c], False, True)
-                nc.scalar.activation(res[c][:, t, :], banks[t][:], ACT.Tanh)
-                if t % 2:
-                    nc.sync.dma_start(out=out_rows[:, t - 1 : t + 1, spans[c]], in_=res[c][:, t - 1 : t + 1, :])
-
-        banks_b = open_redone(1, ["plane_bank%d" % t for t in range(PACK)])
-
-        def fetch(c):
-            span = spans[c]
-            n = span.stop - span.start
-            picks = nb_t[:, span.start // 16 : span.stop // 16]
-            sig = sb("sig%d" % c, [P, PACK - 1, n], F32)
-            z2_planes = sb("z2_planes%d" % c, [P, PACK, n], F32)
-            for t in range(PACK - 1):
-                nc.scalar.activation(sig[:, t, :], windows[t][:].indirect(picks), ACT.Sigmoid, scale=2.0)
-            nc.vector.tensor_tensor(
-                z2_planes[:, V_PLANE, :], windows[V_PLANE][:].indirect(picks), gain_row[:, :n], ALU.mult
-            )
-            return sig, z2_planes
-
-        def quantize_z2(c, sig, z2_planes):
-            span = spans[c]
-            n = span.stop - span.start
-            for t in range(PACK - 1):
-                if c == 2:
-                    nc.scalar.activation(
-                        z2_planes[:, t, :], sig[:, t, :], ACT.Identity,
-                        bias=neg_half_gain[:, t : t + 1], scale=gain[:, t : t + 1],
-                    )
-                else:
-                    nc.vector.tensor_scalar(
-                        z2_planes[:, t, :], sig[:, t, :], 0.5, gain[:, t : t + 1], ALU.subtract, ALU.mult
-                    )
-            zb = sb("z2_bf%d" % c, [P, n * PACK], BF16)
-            nc.vector.tensor_copy(
-                out=zb[:].rearrange("p (a i t) -> p a t i", i=4, t=PACK),
-                in_=z2_planes[:].rearrange("p t (a i) -> p a t i", i=4),
-            )
-            nc.vector.quantize_mx(
-                out=z2_codes[:, span].bitcast(FP8X4), scales=z2_scales[:, span], in_=zb[:]
-            )
-
-        fetched = [fetch(c) for c in range(3)]
-        quantize_z2(0, *fetched[0])
         res = [sb("res%d" % c, [P, PACK, spans[c].stop - spans[c].start], F32) for c in range(3)]
-        for u in range(2):
-            pair = slice(2 * u, 2 * u + 2)
-            bank = psum.tile([P, 2, HALF], F32, name="chunk_bank%d" % u)
-            for a in range(2):
-                mx(bank[:, a, :], w2_codes, w2_scales, 2 * u + a, z2_codes, z2_scales, spans[0], True, True)
-            pre = sb("pre%d" % u, [P, 2, HALF], F32)
-            nc.vector.tensor_tensor(pre[:], bank[:], y_sb[:, pair, spans[0]], ALU.add)
-            nc.scalar.activation(res[0][:, pair, :], pre[:], ACT.Tanh)
-            nc.sync.dma_start(out=out_rows[:, pair, spans[0]], in_=res[0][:, pair, :])
 
-        banks_c = open_redone(2, ["chunk_bank%d" % b for b in (2, 3, 0, 1)])
-        quantize_z2(1, *fetched[1])
-        close_redone(1, banks_b)
-        quantize_z2(2, *fetched[2])
-        close_redone(2, banks_c)
+        first_banks = []
+        for t in range(PACK):
+            bank = psum.tile([P, HALF], F32, name="plane_bank%d" % t)
+            mx(bank[:], w1_codes, w1_scales, t, xq_codes, xq_scales, spans[0], True, False)
+            first_banks.append(bank)
+
+        sig_first = sb("sig_first", [P, PACK - 1, HALF], F32)
+        late = sb("late", [P, 2, 2 * PACK - 1, CHUNK], F32, tag="th1")
+        z2_first = y_and_sig[:, 2:6, halves[0]]
+        sigs = [sig_first[:, :, cols(c, CHUNK)] for c in range(2)] + [late[:, c, PACK:] for c in range(2)]
+        z2_planes = [z2_first[:, :, cols(c, CHUNK)] for c in range(2)] + [late[:, c, :PACK] for c in range(2)]
+
+        def picks(span):
+            return nb_t[:, span.start // 16 : span.stop // 16]
+
+        def fetch_sigmoid(dst, t, span):
+            nc.scalar.activation(dst, windows[t][:].indirect(picks(span)), ACT.Sigmoid, scale=2.0)
+
+        def fetch_plane0(dst, span):
+            nc.vector.tensor_tensor(
+                dst, windows[0][:].indirect(picks(span)), gain_row[:, : span.stop - span.start], ALU.mult
+            )
+
+        def shift_and_gain(dst, src, t):
+            nc.vector.tensor_scalar(dst, src, 0.5, gain[:, t : t + 1], ALU.subtract, ALU.mult)
+
+        for t in range(1, 3):
+            fetch_sigmoid(sig_first[:, t - 1, :], t, halves[0])
+        for c in range(2):
+            fetch_sigmoid(sigs[c][:, 2, :], 3, cols(c, CHUNK))
+        for c in range(2, CHUNKS):
+            for t in range(1, PACK):
+                fetch_sigmoid(sigs[c][:, t - 1, :], t, cols(c, CHUNK))
+
+        z2_bf = sb("z2_bf", [P, S, PACK], BF16)
+
+        def weave_z2(c):
+            nc.vector.tensor_copy(
+                out=z2_bf[:, cols(c, CHUNK), :].rearrange("p (a i) t -> p a t i", i=4),
+                in_=z2_planes[c].rearrange("p t (a i) -> p a t i", i=4),
+            )
+
+        def quantize_z2(c):
+            span = cols(c, CHUNK)
+            nc.vector.quantize_mx(
+                out=z2_codes[:, span].bitcast(FP8X4),
+                scales=z2_scales[:, span],
+                in_=z2_bf[:, span, :].rearrange("p n t -> p (n t)"),
+            )
+
+        def finish_added(c, planes, bank_name):
+            span = cols(c, CHUNK)
+            count = planes.stop - planes.start
+            bank = psum.tile([P, count, CHUNK], F32, name=bank_name)
+            for a in range(count):
+                mx(bank[:, a, :], w2_codes, w2_scales, planes.start + a, z2_codes, z2_scales, span, True, True)
+            pre = sb("pre_" + bank_name, [P, count, CHUNK], F32)
+            nc.vector.tensor_tensor(pre[:], bank[:], y_sb[:, planes, span], ALU.add)
+            nc.scalar.activation(res[c - 1][:, planes, :], pre[:], ACT.Tanh)
+            nc.sync.dma_start(out=out_rows[:, planes, span], in_=res[c - 1][:, planes, :])
+
+        fetch_plane0(z2_first[:, 0, :], halves[0])
+        for t in range(1, 3):
+            shift_and_gain(z2_first[:, t, :], sig_first[:, t - 1, :], t)
+        for c in range(2):
+            shift_and_gain(z2_planes[c][:, 3, :], sigs[c][:, 2, :], 3)
+            weave_z2(c)
+        quantize_z2(0)
+        for t in range(PACK):
+            mx(first_banks[t][:, cols(0, CHUNK)], w2_codes, w2_scales, t, z2_codes, z2_scales, cols(0, CHUNK), False, False)
+        fetch_plane0(z2_planes[2][:, 0, :], cols(2, CHUNK))
+        quantize_z2(1)
+        for t in range(PACK):
+            mx(first_banks[t][:, cols(1, CHUNK)], w2_codes, w2_scales, t, z2_codes, z2_scales, cols(1, CHUNK), False, True)
+        for t in range(1, PACK):
+            shift_and_gain(z2_planes[2][:, t, :], sigs[2][:, t - 1, :], t)
+        weave_z2(2)
+        fetch_plane0(z2_planes[3][:, 0, :], cols(3, CHUNK))
+        quantize_z2(2)
+        for t in range(1, PACK):
+            shift_and_gain(z2_planes[3][:, t, :], sigs[3][:, t - 1, :], t)
+        for t in range(PACK):
+            nc.scalar.activation(res[0][:, t, :], first_banks[t][:], ACT.Tanh)
+            nc.sync.dma_start(out=out_rows[:, t, halves[0]], in_=res[0][:, t, :])
+        weave_z2(3)
+        for u in range(2):
+            finish_added(2, slice(2 * u, 2 * u + 2), "chunk_bank%d" % u)
+        quantize_z2(3)
+        for u in range(2):
+            finish_added(3, slice(2 * u, 2 * u + 2), "chunk_bank%d" % (u + 2))

@@ -60,7 +60,6 @@ def tile_picked_implicit2_none_p_kernel(
 
         nc.gpsimd.memset(xs[:].bitcast(I32), 0)
         nc.vector.memset(warm[:, 0:1], 0.0)
-        nc.scalar.dma_start(out=gain[:], in_=gn.rearrange("(p t) o -> p (t o)", t=PACK))
         nc.sync.dma_start(offs_t[:], offs)
         nc.sync.dma_start(out=w1_raw[:], in_=w1.rearrange("(p j) c -> p j c", j=PACK))
         for r in range(4):
@@ -70,6 +69,7 @@ def tile_picked_implicit2_none_p_kernel(
         )
         w2_rows = w2.rearrange("(p j) c -> p j c", j=PACK)
         nc.sync.dma_start(out=w2_raw[0][:], in_=w2_rows[:, :, cols(0, H // 2)])
+        nc.sync.dma_start(out=gain[:], in_=gn.rearrange("(p t) o -> p (t o)", t=PACK))
         nc.sync.dma_start(out=w2_raw[1][:], in_=w2_rows[:, :, cols(1, H // 2)])
         nc.sync.dma_start(nb_t[:], nb)
         nc.scalar.activation(warm[:, 1:2], warm[:, 0:1], ACT.Sigmoid)
@@ -186,7 +186,9 @@ def tile_picked_implicit2_none_p_kernel(
         nc.vector.tensor_tensor(windows[3][:, halves[0]], h_banks[3][:, halves[0]], y_last[:], ALU.add)
 
         gain_row = sb("gain_row", [P, HALF], F32)
-        nc.scalar.activation(gain_row[:], gain[:, 0:1].to_broadcast([P, HALF]), ACT.Copy, scale=0.5)
+        nc.vector.tensor_scalar(gain_row[:], gain[:, 0:1].to_broadcast([P, HALF]), 0.5, None, ALU.mult)
+        neg_half_gain = sb("neg_half_gain", [P, PACK], F32)
+        nc.vector.tensor_scalar(neg_half_gain[:], gain[:], -0.5, None, ALU.mult)
 
         z2_codes = sb("z2_codes", [P, S], U32)
         z2_scales = sb("z2_scales", [P, S], U8)
@@ -273,7 +275,10 @@ def tile_picked_implicit2_none_p_kernel(
         fetch_plane0(z2_planes[3][:, 0, :], cols(3, CHUNK))
         quantize_z2(2)
         for t in range(1, PACK):
-            shift_and_gain(z2_planes[3][:, t, :], sigs[3][:, t - 1, :], t)
+            nc.scalar.activation(
+                z2_planes[3][:, t, :], sigs[3][:, t - 1, :], ACT.Identity,
+                bias=neg_half_gain[:, t : t + 1], scale=gain[:, t : t + 1],
+            )
         for t in range(PACK):
             nc.scalar.activation(res[0][:, t, :], first_banks[t][:], ACT.Tanh)
             nc.sync.dma_start(out=out_rows[:, t, halves[0]], in_=res[0][:, t, :])

@@ -3,7 +3,7 @@ from contextlib import ExitStack
 import concourse.mybir as mybir
 
 K, T, S, H = 512, 2048, 512, 512
-FLOPS = 3 * 2 * 512 * 512 * 512
+FLOPS = 2 * S * H * (K + 2 * H)
 
 F32 = mybir.dt.float32
 BF16 = mybir.dt.bfloat16
@@ -20,8 +20,11 @@ PACK = 4
 CHUNK = 128
 CHUNKS = S // CHUNK
 HALF = S // 2
+QUADRANT = 32
+LIST_ROWS = 16
+RUN = 4
 W1_SCALAR = 72
-W2_SCALAR = 32
+W2_SCALAR = 48
 
 
 def tile_picked_implicit2_none_p_kernel(
@@ -49,21 +52,19 @@ def tile_picked_implicit2_none_p_kernel(
                 stop=stop,
             )
 
-        offs_t = keep.tile([P, S // 16], U16, name="offs_t")
-        nb_t = keep.tile([P, S // 16], U16, name="nb_t")
+        offs_t = keep.tile([P, S // LIST_ROWS], U16, name="offs_t")
+        nb_t = keep.tile([P, S // LIST_ROWS], U16, name="nb_t")
         w1_raw = sb("w1_raw", [P, PACK, H], F32)
         w2_raw = [sb("w2_raw%d" % u, [P, PACK, H // 2], F32) for u in range(2)]
         xw = sb("xw", [P, T], U32)
         xs = sb("xs", [P, T], U8)
         gain = sb("gain", [P, PACK], F32)
-        warm = sb("warm", [P, 2], F32)
 
         nc.gpsimd.memset(xs[:].bitcast(I32), 0)
-        nc.vector.memset(warm[:, 0:1], 0.0)
         nc.sync.dma_start(offs_t[:], offs)
         nc.sync.dma_start(out=w1_raw[:], in_=w1.rearrange("(p j) c -> p j c", j=PACK))
         for r in range(4):
-            nc.sync.dma_start(out=xs[r:P:32, :].bitcast(I32), in_=x_scales[0, r:16:4, :].bitcast(I32))
+            nc.sync.dma_start(out=xs[r:P:QUADRANT, :].bitcast(I32), in_=x_scales[0, r:16:4, :].bitcast(I32))
         nc.sync.dma_start(
             out=xw[:].bitcast(I32), in_=x_words[0].rearrange("p n r -> p (n r)").bitcast(I32)
         )
@@ -72,7 +73,6 @@ def tile_picked_implicit2_none_p_kernel(
         nc.sync.dma_start(out=gain[:], in_=gn.rearrange("(p t) o -> p (t o)", t=PACK))
         nc.sync.dma_start(out=w2_raw[1][:], in_=w2_rows[:, :, cols(1, H // 2)])
         nc.sync.dma_start(nb_t[:], nb)
-        nc.scalar.activation(warm[:, 1:2], warm[:, 0:1], ACT.Sigmoid)
 
         xq_scales = sb("xq_scales", [P, S], U8)
         nc.vector.tensor_copy(xq_scales[:], xs[:].indirect(offs_t[:]))
@@ -97,7 +97,7 @@ def tile_picked_implicit2_none_p_kernel(
         xq_codes = sb("xq_codes", [P, S], U32, tag="w1_grouped")
         for u in range(2):
             nc.vector.tensor_copy(
-                xq_codes[:, cols(u, HALF)], xw[:].indirect(offs_t[:, cols(u, HALF // 16)])
+                xq_codes[:, cols(u, HALF)], xw[:].indirect(offs_t[:, cols(u, HALF // LIST_ROWS)])
             )
 
         w2_grouped = sb("w2_grouped", [P, PACK, P, PACK], BF16)
@@ -126,15 +126,15 @@ def tile_picked_implicit2_none_p_kernel(
             )
 
         y_banks = []
-        tanh_y = []
+        sig_y = []
         for c in range(CHUNKS):
             bank = psum.tile([P, PACK, CHUNK], F32, name="chunk_bank%d" % c)
             y_banks.append(bank)
             for t in range(PACK):
                 mx(bank[:, t, :], w1_codes, w1_scales, t, xq_codes, xq_scales, cols(c, CHUNK), True, True)
-            th = sb("th%d" % c, [P, CHUNK, PACK], F32)
-            nc.scalar.activation(th[:], bank[:].rearrange("p t n -> p n t"), ACT.Tanh)
-            tanh_y.append(th)
+            woven = sb("sig_y%d" % c, [P, CHUNK, PACK], F32)
+            nc.scalar.activation(woven[:], bank[:].rearrange("p t n -> p n t"), ACT.Sigmoid, scale=2.0)
+            sig_y.append(woven)
         nc.scalar.copy(
             *weave_views(w2_grouped, w2_raw[1], slice(P - W2_SCALAR, P), slice(P // 2 - W2_SCALAR, P // 2))
         )
@@ -142,26 +142,26 @@ def tile_picked_implicit2_none_p_kernel(
         def make_z(c):
             nc.vector.scalar_tensor_tensor(
                 z_bf[:, cols(c, CHUNK * PACK)].rearrange("p (n t) -> p n t", t=PACK),
-                tanh_y[c][:],
+                sig_y[c][:],
                 0.5,
                 gain[:].unsqueeze(1).to_broadcast([P, CHUNK, PACK]),
-                ALU.mult,
+                ALU.subtract,
                 ALU.mult,
             )
 
-        make_z(0)
-        make_z(1)
-        make_z(2)
+        for c in range(CHUNKS - 1):
+            make_z(c)
         nc.vector.tensor_copy(
             *weave_views(w2_grouped, w2_raw[1], slice(P // 2, P - W2_SCALAR), slice(0, P // 2 - W2_SCALAR))
         )
         quantize_z(spans[0])
         quantize_w2(0)
-        make_z(3)
+        make_z(CHUNKS - 1)
         quantize_z(spans[1])
-        y_and_sig = sb("y_and_sig", [P, 6, S], F32, tag="th0")
-        y_sb = y_and_sig[:, 0:PACK, :]
-        y_last = sb("y_last", [P, HALF], F32, tag="th1")
+
+        y_and_z2 = sb("y_and_z2", [P, PACK + 2, S], F32, tag="sig_y0")
+        y_sb = y_and_z2[:, 0:PACK, :]
+        y_last = sb("y_last", [P, HALF], F32, tag="sig_y1")
         for c in range(2):
             nc.scalar.copy(out=y_sb[:, 1:3, cols(c, CHUNK)], in_=y_banks[c][:, 1:3, :])
         for c in range(2, CHUNKS):
@@ -202,13 +202,13 @@ def tile_picked_implicit2_none_p_kernel(
             first_banks.append(bank)
 
         sig_first = sb("sig_first", [P, PACK - 1, HALF], F32)
-        late = sb("late", [P, 2, 2 * PACK - 1, CHUNK], F32, tag="th1")
-        z2_first = y_and_sig[:, 2:6, halves[0]]
+        late = sb("late", [P, 2, 2 * PACK - 1, CHUNK], F32, tag="sig_y1")
+        z2_first = y_and_z2[:, 2 : PACK + 2, halves[0]]
         sigs = [sig_first[:, :, cols(c, CHUNK)] for c in range(2)] + [late[:, c, PACK:] for c in range(2)]
         z2_planes = [z2_first[:, :, cols(c, CHUNK)] for c in range(2)] + [late[:, c, :PACK] for c in range(2)]
 
         def picks(span):
-            return nb_t[:, span.start // 16 : span.stop // 16]
+            return nb_t[:, span.start // LIST_ROWS : span.stop // LIST_ROWS]
 
         def fetch_sigmoid(dst, t, span):
             nc.scalar.activation(dst, windows[t][:].indirect(picks(span)), ACT.Sigmoid, scale=2.0)
@@ -233,8 +233,8 @@ def tile_picked_implicit2_none_p_kernel(
 
         def weave_z2(c):
             nc.vector.tensor_copy(
-                out=z2_bf[:, cols(c, CHUNK), :].rearrange("p (a i) t -> p a t i", i=4),
-                in_=z2_planes[c].rearrange("p t (a i) -> p a t i", i=4),
+                out=z2_bf[:, cols(c, CHUNK), :].rearrange("p (a i) t -> p a t i", i=RUN),
+                in_=z2_planes[c].rearrange("p t (a i) -> p a t i", i=RUN),
             )
 
         def quantize_z2(c):
@@ -245,16 +245,21 @@ def tile_picked_implicit2_none_p_kernel(
                 in_=z2_bf[:, span, :].rearrange("p n t -> p (n t)"),
             )
 
-        def finish_added(c, planes, bank_name):
+        def finish_added(c, u):
             span = cols(c, CHUNK)
-            count = planes.stop - planes.start
-            bank = psum.tile([P, count, CHUNK], F32, name=bank_name)
-            for a in range(count):
-                mx(bank[:, a, :], w2_codes, w2_scales, planes.start + a, z2_codes, z2_scales, span, True, True)
-            pre = sb("pre_" + bank_name, [P, count, CHUNK], F32)
-            nc.vector.tensor_tensor(pre[:], bank[:], y_sb[:, planes, span], ALU.add)
-            nc.scalar.activation(res[c - 1][:, planes, :], pre[:], ACT.Tanh)
-            nc.sync.dma_start(out=out_rows[:, planes, span], in_=res[c - 1][:, planes, :])
+            pair = cols(u, 2)
+            bank = psum.tile([P, 2, CHUNK], F32, name="chunk_bank%d" % (2 * (c - 2) + u))
+            for a in range(2):
+                mx(bank[:, a, :], w2_codes, w2_scales, pair.start + a, z2_codes, z2_scales, span, True, True)
+            pre = sb("pre%d%d" % (c, u), [P, 2, CHUNK], F32)
+            nc.vector.tensor_tensor(pre[:], bank[:], y_sb[:, pair, span], ALU.add)
+            nc.scalar.activation(res[c - 1][:, pair, :], pre[:], ACT.Tanh)
+            nc.sync.dma_start(out=out_rows[:, pair, span], in_=res[c - 1][:, pair, :])
+
+        def add_to_first(c):
+            span = cols(c, CHUNK)
+            for t in range(PACK):
+                mx(first_banks[t][:, span], w2_codes, w2_scales, t, z2_codes, z2_scales, span, False, c == 1)
 
         fetch_plane0(z2_first[:, 0, :], halves[0])
         for t in range(1, 3):
@@ -263,12 +268,10 @@ def tile_picked_implicit2_none_p_kernel(
             shift_and_gain(z2_planes[c][:, 3, :], sigs[c][:, 2, :], 3)
             weave_z2(c)
         quantize_z2(0)
-        for t in range(PACK):
-            mx(first_banks[t][:, cols(0, CHUNK)], w2_codes, w2_scales, t, z2_codes, z2_scales, cols(0, CHUNK), False, False)
+        add_to_first(0)
         fetch_plane0(z2_planes[2][:, 0, :], cols(2, CHUNK))
         quantize_z2(1)
-        for t in range(PACK):
-            mx(first_banks[t][:, cols(1, CHUNK)], w2_codes, w2_scales, t, z2_codes, z2_scales, cols(1, CHUNK), False, True)
+        add_to_first(1)
         for t in range(1, PACK):
             shift_and_gain(z2_planes[2][:, t, :], sigs[2][:, t - 1, :], t)
         weave_z2(2)
@@ -284,7 +287,7 @@ def tile_picked_implicit2_none_p_kernel(
             nc.sync.dma_start(out=out_rows[:, t, halves[0]], in_=res[0][:, t, :])
         weave_z2(3)
         for u in range(2):
-            finish_added(2, slice(2 * u, 2 * u + 2), "chunk_bank%d" % u)
+            finish_added(2, u)
         quantize_z2(3)
         for u in range(2):
-            finish_added(3, slice(2 * u, 2 * u + 2), "chunk_bank%d" % (u + 2))
+            finish_added(3, u)

@@ -24,7 +24,7 @@ QUADRANT = 32
 LIST_ROWS = 16
 RUN = 4
 W1_SCALAR = 72
-W2_SCALAR = 48
+W2_SCALAR = 32
 
 
 def tile_picked_implicit2_none_p_kernel(
@@ -55,23 +55,25 @@ def tile_picked_implicit2_none_p_kernel(
         offs_t = keep.tile([P, S // LIST_ROWS], U16, name="offs_t")
         nb_t = keep.tile([P, S // LIST_ROWS], U16, name="nb_t")
         w1_raw = sb("w1_raw", [P, PACK, H], F32)
-        w2_raw = [sb("w2_raw%d" % u, [P, PACK, H // 2], F32) for u in range(2)]
+        w2_parts = [slice(0, H // 2), slice(H // 2, 3 * H // 4), slice(3 * H // 4, H)]
+        w2_raw = [sb("w2_raw%d" % u, [P, PACK, part.stop - part.start], F32) for u, part in enumerate(w2_parts)]
         xw = sb("xw", [P, T], U32)
         xs = sb("xs", [P, T], U8)
         gain = sb("gain", [P, PACK], F32)
 
         nc.gpsimd.memset(xs[:].bitcast(I32), 0)
-        nc.sync.dma_start(offs_t[:], offs)
         nc.sync.dma_start(out=w1_raw[:], in_=w1.rearrange("(p j) c -> p j c", j=PACK))
+        nc.sync.dma_start(offs_t[:], offs)
         for r in range(4):
             nc.sync.dma_start(out=xs[r:P:QUADRANT, :].bitcast(I32), in_=x_scales[0, r:16:4, :].bitcast(I32))
         nc.sync.dma_start(
             out=xw[:].bitcast(I32), in_=x_words[0].rearrange("p n r -> p (n r)").bitcast(I32)
         )
         w2_rows = w2.rearrange("(p j) c -> p j c", j=PACK)
-        nc.sync.dma_start(out=w2_raw[0][:], in_=w2_rows[:, :, cols(0, H // 2)])
+        nc.sync.dma_start(out=w2_raw[0][:], in_=w2_rows[:, :, w2_parts[0]])
+        nc.sync.dma_start(out=w2_raw[1][:], in_=w2_rows[:, :, w2_parts[1]])
         nc.sync.dma_start(out=gain[:], in_=gn.rearrange("(p t) o -> p (t o)", t=PACK))
-        nc.sync.dma_start(out=w2_raw[1][:], in_=w2_rows[:, :, cols(1, H // 2)])
+        nc.sync.dma_start(out=w2_raw[2][:], in_=w2_rows[:, :, w2_parts[2]])
         nc.sync.dma_start(nb_t[:], nb)
 
         xq_scales = sb("xq_scales", [P, S], U8)
@@ -102,6 +104,7 @@ def tile_picked_implicit2_none_p_kernel(
 
         w2_grouped = sb("w2_grouped", [P, PACK, P, PACK], BF16)
         nc.vector.tensor_copy(*weave_views(w2_grouped, w2_raw[0], slice(0, P // 2), slice(0, P // 2)))
+        nc.vector.tensor_copy(*weave_views(w2_grouped, w2_raw[1], slice(P // 2, 3 * P // 4), slice(0, P // 4)))
 
         z_codes = sb("z_codes", [P, S], U32)
         z_scales = sb("z_scales", [P, S], U8)
@@ -118,11 +121,12 @@ def tile_picked_implicit2_none_p_kernel(
                 in_=z_bf[:, span.start * PACK : span.stop * PACK],
             )
 
-        def quantize_w2(u):
+        def quantize_w2(first, last):
+            span = slice(first * P, (last + 1) * P)
             nc.vector.quantize_mx(
-                out=w2_codes[:, cols(u, 2 * P)].bitcast(FP8X4),
-                scales=w2_scales[:, cols(u, 2 * P)],
-                in_=w2_grouped[:, 2 * u : 2 * u + 2].rearrange("p t m j -> p (t m j)"),
+                out=w2_codes[:, span].bitcast(FP8X4),
+                scales=w2_scales[:, span],
+                in_=w2_grouped[:, first : last + 1].rearrange("p t m j -> p (t m j)"),
             )
 
         y_banks = []
@@ -135,9 +139,7 @@ def tile_picked_implicit2_none_p_kernel(
             woven = sb("sig_y%d" % c, [P, CHUNK, PACK], F32)
             nc.scalar.activation(woven[:], bank[:].rearrange("p t n -> p n t"), ACT.Sigmoid, scale=2.0)
             sig_y.append(woven)
-        nc.scalar.copy(
-            *weave_views(w2_grouped, w2_raw[1], slice(P - W2_SCALAR, P), slice(P // 2 - W2_SCALAR, P // 2))
-        )
+        nc.scalar.copy(*weave_views(w2_grouped, w2_raw[2], slice(3 * P // 4, P), slice(0, P // 4)))
 
         def make_z(c):
             nc.vector.scalar_tensor_tensor(
@@ -149,15 +151,15 @@ def tile_picked_implicit2_none_p_kernel(
                 ALU.mult,
             )
 
-        for c in range(CHUNKS - 1):
+        for c in range(2):
             make_z(c)
-        nc.vector.tensor_copy(
-            *weave_views(w2_grouped, w2_raw[1], slice(P // 2, P - W2_SCALAR), slice(0, P // 2 - W2_SCALAR))
-        )
-        quantize_z(spans[0])
-        quantize_w2(0)
-        make_z(CHUNKS - 1)
-        quantize_z(spans[1])
+        make_z(2)
+        quantize_z(halves[0])
+        make_z(3)
+        quantize_w2(1, 1)
+        quantize_z(halves[1])
+        quantize_w2(0, 0)
+        quantize_w2(2, 3)
 
         y_and_z2 = sb("y_and_z2", [P, PACK + 2, S], F32, tag="sig_y0")
         y_sb = y_and_z2[:, 0:PACK, :]
@@ -168,15 +170,14 @@ def tile_picked_implicit2_none_p_kernel(
             nc.scalar.copy(out=y_sb[:, :, cols(c, CHUNK)], in_=y_banks[c][:])
         for c in range(2):
             nc.scalar.copy(out=y_last[:, cols(c, CHUNK)], in_=y_banks[c][:, 3, :])
-        quantize_z(spans[2])
-        quantize_w2(1)
 
         windows = [sb("window%d" % t, [P, S], F32) for t in range(PACK)]
         h_banks = [psum.tile([P, S], F32, name="plane_bank%d" % t) for t in range(PACK)]
-        for span in spans:
-            mx(h_banks[0][:, span], w1_codes, w1_scales, 0, xq_codes, xq_scales, span, True, False)
+        mx(h_banks[0][:], w1_codes, w1_scales, 0, xq_codes, xq_scales, slice(0, S), True, False)
+        for span in halves:
             mx(h_banks[1][:, span], w2_codes, w2_scales, 1, z_codes, z_scales, span, True, True)
-            mx(h_banks[0][:, span], w2_codes, w2_scales, 0, z_codes, z_scales, span, False, True)
+        for span in halves:
+            mx(h_banks[0][:, span], w2_codes, w2_scales, 0, z_codes, z_scales, span, False, span == halves[1])
         nc.scalar.activation(windows[0][:], h_banks[0][:], ACT.Tanh)
         for t in range(2, PACK):
             mx(h_banks[t][:], w2_codes, w2_scales, t, z_codes, z_scales, slice(0, S), True, True)
@@ -286,8 +287,8 @@ def tile_picked_implicit2_none_p_kernel(
             nc.scalar.activation(res[0][:, t, :], first_banks[t][:], ACT.Tanh)
             nc.sync.dma_start(out=out_rows[:, t, halves[0]], in_=res[0][:, t, :])
         weave_z2(3)
-        for u in range(2):
-            finish_added(2, u)
+        finish_added(2, 0)
         quantize_z2(3)
+        finish_added(2, 1)
         for u in range(2):
             finish_added(3, u)

@@ -172,8 +172,14 @@ def tile_picked_implicit2_none_p_kernel(
             nc.scalar.copy(out=y_last[:, cols(c, CHUNK)], in_=y_banks[c][:, 3, :])
 
         windows = [sb("window%d" % t, [P, S], F32) for t in range(PACK)]
-        h_banks = [psum.tile([P, S], F32, name="plane_bank%d" % t) for t in range(PACK)]
+        h_banks = [
+            psum.tile([P, S], F32, name=("plane_bank%d" if t < 2 else "chunk_bank%d") % t) for t in range(PACK)
+        ]
         mx(h_banks[0][:], w1_codes, w1_scales, 0, xq_codes, xq_scales, slice(0, S), True, False)
+        first_pairs = [psum.tile([P, 2, HALF], F32, name="first_bank%d" % u) for u in range(2)]
+        first_banks = [first_pairs[t // 2][:, t % 2, :] for t in range(PACK)]
+        for t in range(PACK):
+            mx(first_banks[t], w1_codes, w1_scales, t, xq_codes, xq_scales, spans[0], t % 2 == 0, False)
         for span in halves:
             mx(h_banks[1][:, span], w2_codes, w2_scales, 1, z_codes, z_scales, span, True, True)
         for span in halves:
@@ -195,12 +201,6 @@ def tile_picked_implicit2_none_p_kernel(
         z2_scales = sb("z2_scales", [P, S], U8)
         out_rows = out.rearrange("(p t) n -> p t n", t=PACK)
         res = [sb("res%d" % c, [P, PACK, spans[c].stop - spans[c].start], F32) for c in range(3)]
-
-        first_banks = []
-        for t in range(PACK):
-            bank = psum.tile([P, HALF], F32, name="plane_bank%d" % t)
-            mx(bank[:], w1_codes, w1_scales, t, xq_codes, xq_scales, spans[0], True, False)
-            first_banks.append(bank)
 
         sig_first = sb("sig_first", [P, PACK - 1, HALF], F32)
         late = sb("late", [P, 2, 2 * PACK - 1, CHUNK], F32, tag="sig_y1")
@@ -230,11 +230,12 @@ def tile_picked_implicit2_none_p_kernel(
             for t in range(1, PACK):
                 fetch_sigmoid(sigs[c][:, t - 1, :], t, cols(c, CHUNK))
 
-        z2_bf = sb("z2_bf", [P, S, PACK], BF16)
+        z2_bf = {}
 
         def weave_z2(c):
+            z2_bf[c] = sb("z2_bf%d" % c, [P, CHUNK, PACK], BF16, tag="z2_bf%d" % c)
             nc.vector.tensor_copy(
-                out=z2_bf[:, cols(c, CHUNK), :].rearrange("p (a i) t -> p a t i", i=RUN),
+                out=z2_bf[c][:].rearrange("p (a i) t -> p a t i", i=RUN),
                 in_=z2_planes[c].rearrange("p t (a i) -> p a t i", i=RUN),
             )
 
@@ -243,24 +244,28 @@ def tile_picked_implicit2_none_p_kernel(
             nc.vector.quantize_mx(
                 out=z2_codes[:, span].bitcast(FP8X4),
                 scales=z2_scales[:, span],
-                in_=z2_bf[:, span, :].rearrange("p n t -> p (n t)"),
+                in_=z2_bf[c][:].rearrange("p n t -> p (n t)"),
             )
+
+        pres = {}
 
         def finish_added(c, u):
             span = cols(c, CHUNK)
             pair = cols(u, 2)
-            bank = psum.tile([P, 2, CHUNK], F32, name="chunk_bank%d" % (2 * (c - 2) + u))
+            bank = psum.tile([P, 2, CHUNK], F32, name=("chunk_bank%d" if c == 2 else "plane_bank%d") % u)
             for a in range(2):
                 mx(bank[:, a, :], w2_codes, w2_scales, pair.start + a, z2_codes, z2_scales, span, True, True)
-            pre = sb("pre%d%d" % (c, u), [P, 2, CHUNK], F32)
-            nc.vector.tensor_tensor(pre[:], bank[:], y_sb[:, pair, span], ALU.add)
-            nc.scalar.activation(res[c - 1][:, pair, :], pre[:], ACT.Tanh)
+            if u == 0:
+                pres[c] = sb("pre%d" % c, [P, PACK, CHUNK], F32)
+            pre = pres[c][:, pair, :]
+            nc.vector.tensor_tensor(pre, bank[:], y_sb[:, pair, span], ALU.add)
+            nc.scalar.activation(res[c - 1][:, pair, :], pre, ACT.Tanh)
             nc.sync.dma_start(out=out_rows[:, pair, span], in_=res[c - 1][:, pair, :])
 
         def add_to_first(c):
             span = cols(c, CHUNK)
             for t in range(PACK):
-                mx(first_banks[t][:, span], w2_codes, w2_scales, t, z2_codes, z2_scales, span, False, c == 1)
+                mx(first_banks[t][:, span], w2_codes, w2_scales, t, z2_codes, z2_scales, span, False, c == 1 and t % 2 == 1)
 
         fetch_plane0(z2_first[:, 0, :], halves[0])
         for t in range(1, 3):
@@ -284,11 +289,11 @@ def tile_picked_implicit2_none_p_kernel(
                 bias=neg_half_gain[:, t : t + 1], scale=gain[:, t : t + 1],
             )
         for t in range(PACK):
-            nc.scalar.activation(res[0][:, t, :], first_banks[t][:], ACT.Tanh)
+            nc.scalar.activation(res[0][:, t, :], first_banks[t], ACT.Tanh)
             nc.sync.dma_start(out=out_rows[:, t, halves[0]], in_=res[0][:, t, :])
         weave_z2(3)
-        finish_added(2, 0)
         quantize_z2(3)
-        finish_added(2, 1)
+        for u in range(2):
+            finish_added(2, u)
         for u in range(2):
             finish_added(3, u)

@@ -33,6 +33,7 @@ def tile_picked_implicit2_none_p_kernel(
     nc = tc.nc
     with ExitStack() as ctx:
         keep = ctx.enter_context(tc.tile_pool(name="keep", bufs=1))
+        placed = ctx.enter_context(tc.tile_pool(name="placed", bufs=1))
         psum = ctx.enter_context(tc.psum_pool(name="psum", bufs=1))
 
         def sb(name, shape, dtype, tag=None):
@@ -58,7 +59,7 @@ def tile_picked_implicit2_none_p_kernel(
         w2_parts = [slice(0, H // 2), slice(H // 2, 3 * H // 4), slice(3 * H // 4, H)]
         w2_raw = [sb("w2_raw%d" % u, [P, PACK, part.stop - part.start], F32) for u, part in enumerate(w2_parts)]
         xw = sb("xw", [P, T], U32)
-        xs = sb("xs", [P, T], U8)
+        xs = placed.tile([P, T], U8, name="xs", offset=T // 2, align_bytes=64)
         gain = sb("gain", [P, PACK], F32)
 
         nc.gpsimd.memset(xs[:].bitcast(I32), 0)
@@ -88,7 +89,7 @@ def tile_picked_implicit2_none_p_kernel(
         w1_grouped = sb("w1_grouped", [P, PACK, P, PACK], BF16)
         nc.scalar.copy(*weave_views(w1_grouped, w1_raw, slice(0, W1_SCALAR), slice(0, W1_SCALAR)))
         nc.vector.tensor_copy(*weave_views(w1_grouped, w1_raw, slice(W1_SCALAR, P), slice(W1_SCALAR, P)))
-        w1_codes = sb("w1_codes", [P, H], U32, tag="xs")
+        w1_codes = placed.tile([P, H], U32, name="w1_codes", offset=0, align_bytes=64)
         w1_scales = sb("w1_scales", [P, H], U8)
         nc.vector.quantize_mx(
             out=w1_codes[:].bitcast(FP8X4),
@@ -96,7 +97,7 @@ def tile_picked_implicit2_none_p_kernel(
             in_=w1_grouped[:].rearrange("p t m j -> p (t m j)"),
         )
 
-        xq_codes = sb("xq_codes", [P, S], U32, tag="w1_grouped")
+        xq_codes = placed.tile([P, S], U32, name="xq_codes", offset=4 * H, align_bytes=64)
         for u in range(2):
             nc.vector.tensor_copy(
                 xq_codes[:, cols(u, HALF)], xw[:].indirect(offs_t[:, cols(u, HALF // LIST_ROWS)])
@@ -156,9 +157,8 @@ def tile_picked_implicit2_none_p_kernel(
         make_z(2)
         quantize_z(halves[0])
         make_z(3)
-        quantize_w2(1, 1)
+        quantize_w2(0, 1)
         quantize_z(halves[1])
-        quantize_w2(0, 0)
         quantize_w2(2, 3)
 
         y_and_z2 = sb("y_and_z2", [P, PACK + 2, S], F32, tag="sig_y0")

@@ -82,8 +82,10 @@ def tile_picked_implicit2_none_p_kernel(
 
         def weave_views(grouped, raw, m_dst, m_src):
             return (
-                grouped[:].rearrange("p t m j -> p m j t")[:, m_dst],
-                raw[:].rearrange("p j (m t) -> p m j t", t=PACK)[:, m_src],
+                grouped[:, :, m_dst, :].rearrange("p t (a b) j -> p a j t b", b=2),
+                raw[:].rearrange("p j (m t) -> p j m t", t=PACK)[:, :, m_src, :].rearrange(
+                    "p j (a b) t -> p a j t b", b=2
+                ),
             )
 
         w1_grouped = sb("w1_grouped", [P, PACK, P, PACK], BF16)

@@ -100,9 +100,9 @@ def tile_picked_implicit2_none_p_kernel(
         )
 
         xq_codes = placed.tile([P, S], U32, name="xq_codes", offset=4 * H, align_bytes=64)
-        for u in range(2):
+        for span in [cols(0, CHUNK), cols(1, CHUNK), cols(1, HALF)]:
             nc.vector.tensor_copy(
-                xq_codes[:, cols(u, HALF)], xw[:].indirect(offs_t[:, cols(u, HALF // LIST_ROWS)])
+                xq_codes[:, span], xw[:].indirect(offs_t[:, span.start // LIST_ROWS : span.stop // LIST_ROWS])
             )
 
         w2_grouped = sb("w2_grouped", [P, PACK, P, PACK], BF16)

@@ -163,15 +163,14 @@ def tile_picked_implicit2_none_p_kernel(
         quantize_z(halves[1])
         quantize_w2(2, 3)
 
-        y_and_z2 = sb("y_and_z2", [P, PACK + 2, S], F32, tag="sig_y0")
-        y_sb = y_and_z2[:, 0:PACK, :]
-        y_last = sb("y_last", [P, HALF], F32, tag="sig_y1")
+        y_rows = sb("y_rows", [P, PACK, 2, 3, CHUNK], F32, tag="sig_y0")
+        y_sb = y_rows[:, :, :, 1:3, :]
         for c in range(2):
-            nc.scalar.copy(out=y_sb[:, 1:3, cols(c, CHUNK)], in_=y_banks[c][:, 1:3, :])
+            nc.scalar.copy(out=y_sb[:, 1:3, 0, c, :], in_=y_banks[c][:, 1:3, :])
         for c in range(2, CHUNKS):
-            nc.scalar.copy(out=y_sb[:, :, cols(c, CHUNK)], in_=y_banks[c][:])
+            nc.scalar.copy(out=y_sb[:, :, 1, c - 2, :], in_=y_banks[c][:])
         for c in range(2):
-            nc.scalar.copy(out=y_last[:, cols(c, CHUNK)], in_=y_banks[c][:, 3, :])
+            nc.scalar.copy(out=y_sb[:, 3, 0, c, :], in_=y_banks[c][:, 3, :])
 
         windows = [sb("window%d" % t, [P, S], F32) for t in range(PACK)]
         h_banks = [
@@ -189,10 +188,13 @@ def tile_picked_implicit2_none_p_kernel(
         nc.scalar.activation(windows[0][:], h_banks[0][:], ACT.Tanh)
         for t in range(2, PACK):
             mx(h_banks[t][:], w2_codes, w2_scales, t, z_codes, z_scales, slice(0, S), True, True)
-        for t in range(1, 3):
-            nc.vector.tensor_tensor(windows[t][:], h_banks[t][:], y_sb[:, t, :], ALU.add)
-        nc.vector.tensor_tensor(windows[3][:, halves[1]], h_banks[3][:, halves[1]], y_sb[:, 3, halves[1]], ALU.add)
-        nc.vector.tensor_tensor(windows[3][:, halves[0]], h_banks[3][:, halves[0]], y_last[:], ALU.add)
+        for t in range(1, PACK):
+            nc.vector.tensor_tensor(
+                windows[t][:].rearrange("p (u n) -> p u n", u=2),
+                h_banks[t][:].rearrange("p (u n) -> p u n", u=2),
+                y_sb[:, t].rearrange("p u c n -> p u (c n)"),
+                ALU.add,
+            )
 
         gain_row = sb("gain_row", [P, HALF], F32)
         nc.vector.tensor_scalar(gain_row[:], gain[:, 0:1].to_broadcast([P, HALF]), 0.5, None, ALU.mult)
@@ -202,13 +204,18 @@ def tile_picked_implicit2_none_p_kernel(
         z2_codes = sb("z2_codes", [P, S], U32)
         z2_scales = sb("z2_scales", [P, S], U8)
         out_rows = out.rearrange("(p t) n -> p t n", t=PACK)
-        res = [sb("res%d" % c, [P, PACK, spans[c].stop - spans[c].start], F32) for c in range(3)]
+        res = [sb("res%d" % u, [P, PACK, HALF], F32) for u in range(2)]
 
-        sig_first = sb("sig_first", [P, PACK - 1, HALF], F32)
-        late = sb("late", [P, 2, 2 * PACK - 1, CHUNK], F32, tag="sig_y1")
-        z2_first = y_and_z2[:, 2 : PACK + 2, halves[0]]
-        sigs = [sig_first[:, :, cols(c, CHUNK)] for c in range(2)] + [late[:, c, PACK:] for c in range(2)]
-        z2_planes = [z2_first[:, :, cols(c, CHUNK)] for c in range(2)] + [late[:, c, :PACK] for c in range(2)]
+        pitch = HALF + CHUNK
+        z2_area = sb("z2_area", [P, CHUNK + (PACK + 1) * pitch], F32)
+        z2_rows = z2_area[:, CHUNK:].rearrange("p (r x) -> p r x", x=pitch)[:, :, 0:HALF]
+        sig_first = [sb("sig_first1", [P, HALF], F32)[:], z2_area[:, cols(0, HALF)], z2_area[:, cols(1, HALF)]]
+        y_row3 = y_rows[:, 3].rearrange("p u c n -> p (u c n)")
+        sig_late = [y_row3[:, cols(t, HALF)] for t in range(2)] + [sb("sig_late3", [P, HALF], F32)]
+        z2_first = z2_rows[:, 1 : PACK + 1, :]
+        z2_late = z2_rows[:, 0:PACK, :]
+        z2_planes = [z2_first, None] + [z2_late[:, :, cols(c, CHUNK)] for c in range(2)]
+        z2_spans = [halves[0], None, cols(2, CHUNK), cols(3, CHUNK)]
 
         def picks(span):
             return nb_t[:, span.start // LIST_ROWS : span.stop // LIST_ROWS]
@@ -224,78 +231,67 @@ def tile_picked_implicit2_none_p_kernel(
         def shift_and_gain(dst, src, t):
             nc.vector.tensor_scalar(dst, src, 0.5, gain[:, t : t + 1], ALU.subtract, ALU.mult)
 
+        for t in range(1, PACK):
+            fetch_sigmoid(sig_first[t - 1], t, halves[0])
+
+        def scalar_shift_and_gain(dst, src, t):
+            nc.scalar.activation(
+                dst, src, ACT.Identity, bias=neg_half_gain[:, t : t + 1], scale=gain[:, t : t + 1]
+            )
+
         for t in range(1, 3):
-            fetch_sigmoid(sig_first[:, t - 1, :], t, halves[0])
-        for c in range(2):
-            fetch_sigmoid(sigs[c][:, 2, :], 3, cols(c, CHUNK))
-        for c in range(2, CHUNKS):
-            for t in range(1, PACK):
-                fetch_sigmoid(sigs[c][:, t - 1, :], t, cols(c, CHUNK))
+            fetch_sigmoid(sig_late[t - 1], t, halves[1])
+        fetch_sigmoid(sig_late[2][:, cols(0, CHUNK)], 3, cols(2, CHUNK))
+        fetch_sigmoid(sig_late[2][:, cols(1, CHUNK)], 3, cols(3, CHUNK))
 
         z2_bf = {}
 
         def weave_z2(c):
-            z2_bf[c] = sb("z2_bf%d" % c, [P, CHUNK, PACK], BF16, tag="z2_bf%d" % c)
+            z2_bf[c] = sb("z2_bf%d" % c, [P, z2_spans[c].stop - z2_spans[c].start, PACK], BF16)
             nc.vector.tensor_copy(
                 out=z2_bf[c][:].rearrange("p (a i) t -> p a t i", i=RUN),
                 in_=z2_planes[c].rearrange("p t (a i) -> p a t i", i=RUN),
             )
 
         def quantize_z2(c):
-            span = cols(c, CHUNK)
+            span = z2_spans[c]
             nc.vector.quantize_mx(
                 out=z2_codes[:, span].bitcast(FP8X4),
                 scales=z2_scales[:, span],
                 in_=z2_bf[c][:].rearrange("p n t -> p (n t)"),
             )
 
-        pres = {}
-
-        def finish_added(c, u):
-            span = cols(c, CHUNK)
-            pair = cols(u, 2)
-            bank = psum.tile([P, 2, CHUNK], F32, name=("chunk_bank%d" if c == 2 else "plane_bank%d") % u)
-            for a in range(2):
-                mx(bank[:, a, :], w2_codes, w2_scales, pair.start + a, z2_codes, z2_scales, span, True, True)
-            if u == 0:
-                pres[c] = sb("pre%d" % c, [P, PACK, CHUNK], F32)
-            pre = pres[c][:, pair, :]
-            nc.vector.tensor_tensor(pre, bank[:], y_sb[:, pair, span], ALU.add)
-            nc.scalar.activation(res[c - 1][:, pair, :], pre, ACT.Tanh)
-            nc.sync.dma_start(out=out_rows[:, pair, span], in_=res[c - 1][:, pair, :])
-
-        def add_to_first(c):
-            span = cols(c, CHUNK)
-            for t in range(PACK):
-                mx(first_banks[t][:, span], w2_codes, w2_scales, t, z2_codes, z2_scales, span, False, c == 1 and t % 2 == 1)
+        def finish_added(t):
+            bank = psum.tile([P, HALF], F32, name=("chunk_bank%d" if t < 2 else "plane_bank%d") % (t % 2))
+            if t == 0:
+                for c in range(2):
+                    mx(bank[:, cols(c, CHUNK)], w2_codes, w2_scales, t, z2_codes, z2_scales, cols(2 + c, CHUNK), True, True)
+            else:
+                mx(bank[:], w2_codes, w2_scales, t, z2_codes, z2_scales, halves[1], True, True)
+            pre = sb("pre%d" % t, [P, HALF], F32)
+            nc.vector.tensor_tensor(pre[:], bank[:], y_sb[:, t, 1].rearrange("p c n -> p (c n)"), ALU.add)
+            nc.scalar.activation(res[1][:, t, :], pre[:], ACT.Tanh)
+            nc.sync.dma_start(out=out_rows[:, t, halves[1]], in_=res[1][:, t, :])
 
         fetch_plane0(z2_first[:, 0, :], halves[0])
-        for t in range(1, 3):
-            shift_and_gain(z2_first[:, t, :], sig_first[:, t - 1, :], t)
-        for c in range(2):
-            shift_and_gain(z2_planes[c][:, 3, :], sigs[c][:, 2, :], 3)
-            weave_z2(c)
-        quantize_z2(0)
-        add_to_first(0)
+        for t in range(1, PACK):
+            shift_and_gain(z2_first[:, t, :], sig_first[t - 1], t)
         fetch_plane0(z2_planes[2][:, 0, :], cols(2, CHUNK))
-        quantize_z2(1)
-        add_to_first(1)
-        for t in range(1, PACK):
-            shift_and_gain(z2_planes[2][:, t, :], sigs[2][:, t - 1, :], t)
-        weave_z2(2)
+        weave_z2(0)
+        scalar_shift_and_gain(z2_late[:, 1, :], sig_late[0], 1)
         fetch_plane0(z2_planes[3][:, 0, :], cols(3, CHUNK))
+        quantize_z2(0)
+        for t in range(PACK):
+            mx(first_banks[t], w2_codes, w2_scales, t, z2_codes, z2_scales, halves[0], False, t % 2 == 1)
+        shift_and_gain(z2_planes[2][:, 3, :], sig_late[2][:, cols(0, CHUNK)], 3)
+        shift_and_gain(z2_late[:, 2, :], sig_late[1], 2)
+        weave_z2(2)
         quantize_z2(2)
-        for t in range(1, PACK):
-            nc.scalar.activation(
-                z2_planes[3][:, t, :], sigs[3][:, t - 1, :], ACT.Identity,
-                bias=neg_half_gain[:, t : t + 1], scale=gain[:, t : t + 1],
-            )
+        scalar_shift_and_gain(z2_planes[3][:, 3, :], sig_late[2][:, cols(1, CHUNK)], 3)
         for t in range(PACK):
             nc.scalar.activation(res[0][:, t, :], first_banks[t], ACT.Tanh)
             nc.sync.dma_start(out=out_rows[:, t, halves[0]], in_=res[0][:, t, :])
         weave_z2(3)
         quantize_z2(3)
-        for u in range(2):
-            finish_added(2, u)
-        for u in range(2):
-            finish_added(3, u)
+        for t in range(PACK):
+            finish_added(t)

@@ -206,15 +206,16 @@ def tile_picked_implicit2_none_p_kernel(
         out_rows = out.rearrange("(p t) n -> p t n", t=PACK)
         res = [sb("res%d" % u, [P, PACK, HALF], F32) for u in range(2)]
 
-        pitch = HALF + CHUNK
-        z2_area = sb("z2_area", [P, CHUNK + (PACK + 1) * pitch], F32)
-        z2_rows = z2_area[:, CHUNK:].rearrange("p (r x) -> p r x", x=pitch)[:, :, 0:HALF]
+        z2_area = sb("z2_area", [P, 12 * CHUNK], F32)
+
+        def area(first, count, planes):
+            return z2_area[:, first * CHUNK : (first + count) * CHUNK].rearrange("p (t n) -> p t n", t=planes)
+
         sig_first = [sb("sig_first1", [P, HALF], F32)[:], z2_area[:, cols(0, HALF)], z2_area[:, cols(1, HALF)]]
         y_row3 = y_rows[:, 3].rearrange("p u c n -> p (u c n)")
         sig_late = [y_row3[:, cols(t, HALF)] for t in range(2)] + [sb("sig_late3", [P, HALF], F32)]
-        z2_first = z2_rows[:, 1 : PACK + 1, :]
-        z2_late = z2_rows[:, 0:PACK, :]
-        z2_planes = [z2_first, None] + [z2_late[:, :, cols(c, CHUNK)] for c in range(2)]
+        z2_first = area(4, 8, PACK)
+        z2_planes = [z2_first, None, area(0, 8, PACK)[:, :, CHUNK:], area(8, 4, PACK)]
         z2_spans = [halves[0], None, cols(2, CHUNK), cols(3, CHUNK)]
 
         def picks(span):
@@ -254,11 +255,12 @@ def tile_picked_implicit2_none_p_kernel(
             )
 
         def quantize_z2(c):
-            span = z2_spans[c]
+            span = cols(c, CHUNK)
+            woven = z2_bf[0][:, span, :] if c < 2 else z2_bf[c][:]
             nc.vector.quantize_mx(
                 out=z2_codes[:, span].bitcast(FP8X4),
                 scales=z2_scales[:, span],
-                in_=z2_bf[c][:].rearrange("p n t -> p (n t)"),
+                in_=woven.rearrange("p n t -> p (n t)"),
             )
 
         def finish_added(t):
@@ -278,16 +280,21 @@ def tile_picked_implicit2_none_p_kernel(
             shift_and_gain(z2_first[:, t, :], sig_first[t - 1], t)
         fetch_plane0(z2_planes[2][:, 0, :], cols(2, CHUNK))
         weave_z2(0)
-        scalar_shift_and_gain(z2_late[:, 1, :], sig_late[0], 1)
+        shift_and_gain(z2_planes[2][:, 1, :], sig_late[0][:, cols(0, CHUNK)], 1)
+        for c in range(2):
+            quantize_z2(c)
+            span = cols(c, CHUNK)
+            for t in range(2):
+                mx(first_banks[t][:, span], w2_codes, w2_scales, t, z2_codes, z2_scales, span, False, c == 1 and t == 1)
+        for t in range(2, PACK):
+            mx(first_banks[t], w2_codes, w2_scales, t, z2_codes, z2_scales, halves[0], False, t == 3)
+        for t in range(2, PACK):
+            shift_and_gain(z2_planes[2][:, t, :], sig_late[t - 1][:, cols(0, CHUNK)], t)
         fetch_plane0(z2_planes[3][:, 0, :], cols(3, CHUNK))
-        quantize_z2(0)
-        for t in range(PACK):
-            mx(first_banks[t], w2_codes, w2_scales, t, z2_codes, z2_scales, halves[0], False, t % 2 == 1)
-        shift_and_gain(z2_planes[2][:, 3, :], sig_late[2][:, cols(0, CHUNK)], 3)
-        shift_and_gain(z2_late[:, 2, :], sig_late[1], 2)
         weave_z2(2)
         quantize_z2(2)
-        scalar_shift_and_gain(z2_planes[3][:, 3, :], sig_late[2][:, cols(1, CHUNK)], 3)
+        for t in range(1, PACK):
+            scalar_shift_and_gain(z2_planes[3][:, t, :], sig_late[t - 1][:, cols(1, CHUNK)], t)
         for t in range(PACK):
             nc.scalar.activation(res[0][:, t, :], first_banks[t], ACT.Tanh)
             nc.sync.dma_start(out=out_rows[:, t, halves[0]], in_=res[0][:, t, :])

@@ -24,7 +24,6 @@ QUADRANT = 32
 LIST_ROWS = 16
 RUN = 4
 W1_SCALAR = 72
-W2_SCALAR = 32
 
 
 def tile_picked_implicit2_none_p_kernel(
@@ -39,19 +38,31 @@ def tile_picked_implicit2_none_p_kernel(
         def sb(name, shape, dtype, tag=None):
             return keep.tile(shape, dtype, name=name, tag=tag or name, align_bytes=64)
 
+        def bank(name, shape, tag):
+            return psum.tile(shape, F32, name=name, tag=tag)
+
         def cols(i, width):
             return slice(i * width, (i + 1) * width)
 
-        def mx(dst, w_codes, w_scales, t, a_codes, a_scales, span, start, stop):
+        def picks(lists, span):
+            return lists[:, span.start // LIST_ROWS : span.stop // LIST_ROWS]
+
+        def mx(dst, weight, t, nodes, span, start, stop):
             nc.tensor.matmul_mx(
                 out=dst,
-                lhsT=w_codes[:, cols(t, P)].bitcast(FP8X4),
-                lhsT_scale=w_scales[:, cols(t, P)],
-                rhs=a_codes[:, span].bitcast(FP8X4),
-                rhs_scale=a_scales[:, span],
+                lhsT=weight[0][:, cols(t, P)].bitcast(FP8X4),
+                lhsT_scale=weight[1][:, cols(t, P)],
+                rhs=nodes[0][:, span].bitcast(FP8X4),
+                rhs_scale=nodes[1][:, span],
                 start=start,
                 stop=stop,
             )
+
+        def quantize(dst, span, woven):
+            nc.vector.quantize_mx(out=dst[0][:, span].bitcast(FP8X4), scales=dst[1][:, span], in_=woven)
+
+        halves = [cols(u, HALF) for u in range(2)]
+        every = slice(0, S)
 
         offs_t = keep.tile([P, S // LIST_ROWS], U16, name="offs_t")
         nb_t = keep.tile([P, S // LIST_ROWS], U16, name="nb_t")
@@ -67,9 +78,7 @@ def tile_picked_implicit2_none_p_kernel(
         nc.sync.dma_start(offs_t[:], offs)
         for r in range(4):
             nc.sync.dma_start(out=xs[r:P:QUADRANT, :].bitcast(I32), in_=x_scales[0, r:16:4, :].bitcast(I32))
-        nc.sync.dma_start(
-            out=xw[:].bitcast(I32), in_=x_words[0].rearrange("p n r -> p (n r)").bitcast(I32)
-        )
+        nc.sync.dma_start(out=xw[:].bitcast(I32), in_=x_words[0].rearrange("p n r -> p (n r)").bitcast(I32))
         w2_rows = w2.rearrange("(p j) c -> p j c", j=PACK)
         nc.sync.dma_start(out=w2_raw[0][:], in_=w2_rows[:, :, w2_parts[0]])
         nc.sync.dma_start(out=w2_raw[1][:], in_=w2_rows[:, :, w2_parts[1]])
@@ -91,62 +100,46 @@ def tile_picked_implicit2_none_p_kernel(
         w1_grouped = sb("w1_grouped", [P, PACK, P, PACK], BF16)
         nc.scalar.copy(*weave_views(w1_grouped, w1_raw, slice(0, W1_SCALAR), slice(0, W1_SCALAR)))
         nc.vector.tensor_copy(*weave_views(w1_grouped, w1_raw, slice(W1_SCALAR, P), slice(W1_SCALAR, P)))
-        w1_codes = placed.tile([P, H], U32, name="w1_codes", offset=0, align_bytes=64)
-        w1_scales = sb("w1_scales", [P, H], U8)
-        nc.vector.quantize_mx(
-            out=w1_codes[:].bitcast(FP8X4),
-            scales=w1_scales[:],
-            in_=w1_grouped[:].rearrange("p t m j -> p (t m j)"),
-        )
+        w1q = (placed.tile([P, H], U32, name="w1_codes", offset=0, align_bytes=64), sb("w1_scales", [P, H], U8))
+        quantize(w1q, slice(0, H), w1_grouped[:].rearrange("p t m j -> p (t m j)"))
 
-        xq_codes = placed.tile([P, S], U32, name="xq_codes", offset=4 * H, align_bytes=64)
-        for span in [cols(0, CHUNK), cols(1, CHUNK), cols(1, HALF)]:
-            nc.vector.tensor_copy(
-                xq_codes[:, span], xw[:].indirect(offs_t[:, span.start // LIST_ROWS : span.stop // LIST_ROWS])
-            )
+        xq = (placed.tile([P, S], U32, name="xq_codes", offset=4 * H, align_bytes=64), xq_scales)
+        for span in [cols(0, CHUNK), cols(1, CHUNK), halves[1]]:
+            nc.vector.tensor_copy(xq[0][:, span], xw[:].indirect(picks(offs_t, span)))
 
         w2_grouped = sb("w2_grouped", [P, PACK, P, PACK], BF16)
         nc.vector.tensor_copy(*weave_views(w2_grouped, w2_raw[0], slice(0, P // 2), slice(0, P // 2)))
         nc.vector.tensor_copy(*weave_views(w2_grouped, w2_raw[1], slice(P // 2, 3 * P // 4), slice(0, P // 4)))
 
-        z_codes = sb("z_codes", [P, S], U32)
-        z_scales = sb("z_scales", [P, S], U8)
-        z_bf = sb("z_bf", [P, S * PACK], BF16)
-        w2_codes = sb("w2_codes", [P, H], U32)
-        w2_scales = sb("w2_scales", [P, H], U8)
-        halves = [cols(u, HALF) for u in range(2)]
-        spans = [halves[0], cols(2, CHUNK), cols(3, CHUNK)]
-
-        def quantize_z(span):
-            nc.vector.quantize_mx(
-                out=z_codes[:, span].bitcast(FP8X4),
-                scales=z_scales[:, span],
-                in_=z_bf[:, span.start * PACK : span.stop * PACK],
-            )
-
-        def quantize_w2(first, last):
-            span = slice(first * P, (last + 1) * P)
-            nc.vector.quantize_mx(
-                out=w2_codes[:, span].bitcast(FP8X4),
-                scales=w2_scales[:, span],
-                in_=w2_grouped[:, first : last + 1].rearrange("p t m j -> p (t m j)"),
-            )
-
         y_banks = []
         sig_y = []
         for c in range(CHUNKS):
-            bank = psum.tile([P, PACK, CHUNK], F32, name="chunk_bank%d" % c)
-            y_banks.append(bank)
+            y_banks.append(bank("y%d" % c, [P, PACK, CHUNK], "bank%d" % c))
             for t in range(PACK):
-                mx(bank[:, t, :], w1_codes, w1_scales, t, xq_codes, xq_scales, cols(c, CHUNK), True, True)
-            woven = sb("sig_y%d" % c, [P, CHUNK, PACK], F32)
-            nc.scalar.activation(woven[:], bank[:].rearrange("p t n -> p n t"), ACT.Sigmoid, scale=2.0)
-            sig_y.append(woven)
+                mx(y_banks[c][:, t, :], w1q, t, xq, cols(c, CHUNK), True, True)
+            sig_y.append(sb("sig_y%d" % c, [P, CHUNK, PACK], F32))
+            nc.scalar.activation(sig_y[c][:], y_banks[c][:].rearrange("p t n -> p n t"), ACT.Sigmoid, scale=2.0)
         nc.scalar.copy(*weave_views(w2_grouped, w2_raw[2], slice(3 * P // 4, P), slice(0, P // 4)))
+
+        h_banks = [bank("h0", [P, S], "bank4")]
+        mx(h_banks[0][:], w1q, 0, xq, every, True, False)
+        pair = bank("out_pair", [P, 2, HALF], "bank5")
+        remade = {
+            (0, 3): bank("out_first3", [P, HALF], "bank6")[:],
+            (0, 0): pair[:, 0, :],
+            (0, 2): pair[:, 1, :],
+            (1, 0): bank("out_late0", [P, HALF], "bank7")[:],
+        }
+        for (u, t), dst in remade.items():
+            mx(dst, w1q, t, xq, halves[u], (u, t) != (0, 2), False)
+
+        zq = (sb("z_codes", [P, S], U32), sb("z_scales", [P, S], U8))
+        w2q = (sb("w2_codes", [P, H], U32), sb("w2_scales", [P, H], U8))
+        z_bf = sb("z_bf", [P, S, PACK], BF16)
 
         def make_z(c):
             nc.vector.scalar_tensor_tensor(
-                z_bf[:, cols(c, CHUNK * PACK)].rearrange("p (n t) -> p n t", t=PACK),
+                z_bf[:, cols(c, CHUNK), :],
                 sig_y[c][:],
                 0.5,
                 gain[:].unsqueeze(1).to_broadcast([P, CHUNK, PACK]),
@@ -154,151 +147,147 @@ def tile_picked_implicit2_none_p_kernel(
                 ALU.mult,
             )
 
-        for c in range(2):
+        def quantize_z(u):
+            quantize(zq, halves[u], z_bf[:, halves[u], :].rearrange("p n t -> p (n t)"))
+
+        def quantize_w2(u):
+            quantize(w2q, halves[u], w2_grouped[:, 2 * u : 2 * u + 2].rearrange("p t m j -> p (t m j)"))
+
+        for c in range(3):
             make_z(c)
-        make_z(2)
-        quantize_z(halves[0])
+        quantize_z(0)
         make_z(3)
-        quantize_w2(0, 1)
-        quantize_z(halves[1])
-        quantize_w2(2, 3)
+        quantize_w2(0)
+        quantize_z(1)
+        quantize_w2(1)
 
-        y_rows = sb("y_rows", [P, PACK, 2, 3, CHUNK], F32, tag="sig_y0")
+        y_rows = sb("y_rows", [P, PACK - 1, 2, 3, CHUNK], F32, tag="sig_y0")
         y_sb = y_rows[:, :, :, 1:3, :]
-        for c in range(2):
-            nc.scalar.copy(out=y_sb[:, 1:3, 0, c, :], in_=y_banks[c][:, 1:3, :])
-        for c in range(2, CHUNKS):
-            nc.scalar.copy(out=y_sb[:, :, 1, c - 2, :], in_=y_banks[c][:])
-        for c in range(2):
-            nc.scalar.copy(out=y_sb[:, 3, 0, c, :], in_=y_banks[c][:, 3, :])
+        for c in range(CHUNKS):
+            nc.scalar.copy(out=y_sb[:, :, c // 2, c % 2, :], in_=y_banks[c][:, 1:PACK, :])
 
-        windows = [sb("window%d" % t, [P, S], F32) for t in range(PACK)]
-        h_banks = [
-            psum.tile([P, S], F32, name=("plane_bank%d" if t < 2 else "chunk_bank%d") % t) for t in range(PACK)
-        ]
-        mx(h_banks[0][:], w1_codes, w1_scales, 0, xq_codes, xq_scales, slice(0, S), True, False)
-        first_pairs = [psum.tile([P, 2, HALF], F32, name="first_bank%d" % u) for u in range(2)]
-        first_banks = [first_pairs[t // 2][:, t % 2, :] for t in range(PACK)]
-        for t in range(PACK):
-            mx(first_banks[t], w1_codes, w1_scales, t, xq_codes, xq_scales, spans[0], t % 2 == 0, False)
+        h_banks += [bank("h%d" % t, [P, S], "bank%d" % (t - 1)) for t in range(1, PACK)]
         for span in halves:
-            mx(h_banks[1][:, span], w2_codes, w2_scales, 1, z_codes, z_scales, span, True, True)
+            mx(h_banks[1][:, span], w2q, 1, zq, span, True, True)
         for span in halves:
-            mx(h_banks[0][:, span], w2_codes, w2_scales, 0, z_codes, z_scales, span, False, span == halves[1])
-        nc.scalar.activation(windows[0][:], h_banks[0][:], ACT.Tanh)
+            mx(h_banks[0][:, span], w2q, 0, zq, span, False, span == halves[1])
         for t in range(2, PACK):
-            mx(h_banks[t][:], w2_codes, w2_scales, t, z_codes, z_scales, slice(0, S), True, True)
+            mx(h_banks[t][:], w2q, t, zq, every, True, True)
+        windows = [sb("window%d" % t, [P, S], F32) for t in range(PACK)]
+        h0 = sb("h0_sb", [P, S], F32)
+        nc.scalar.activation(h0[:], h_banks[0][:], ACT.Tanh)
+        neg_half_gain = sb("neg_half_gain", [P, PACK], F32, tag="w2_grouped")
+        nc.gpsimd.tensor_scalar(neg_half_gain[:], gain[:], -0.5, 1.0, ALU.mult, ALU.mult)
+        nc.gpsimd.tensor_scalar(windows[0][:], h0[:], gain[:, 0:1], 0.5, ALU.mult, ALU.mult)
         for t in range(1, PACK):
             nc.vector.tensor_tensor(
                 windows[t][:].rearrange("p (u n) -> p u n", u=2),
                 h_banks[t][:].rearrange("p (u n) -> p u n", u=2),
-                y_sb[:, t].rearrange("p u c n -> p u (c n)"),
+                y_sb[:, t - 1].rearrange("p u c n -> p u (c n)"),
                 ALU.add,
             )
 
-        gain_row = sb("gain_row", [P, HALF], F32)
-        nc.vector.tensor_scalar(gain_row[:], gain[:, 0:1].to_broadcast([P, HALF]), 0.5, None, ALU.mult)
-        neg_half_gain = sb("neg_half_gain", [P, PACK], F32)
-        nc.vector.tensor_scalar(neg_half_gain[:], gain[:], -0.5, None, ALU.mult)
+        area = sb("area", [P, 12 * CHUNK], F32)
 
-        z2_codes = sb("z2_codes", [P, S], U32)
-        z2_scales = sb("z2_scales", [P, S], U8)
-        out_rows = out.rearrange("(p t) n -> p t n", t=PACK)
-        res = [sb("res%d" % u, [P, PACK, HALF], F32) for u in range(2)]
+        def part(first, count):
+            return area[:, first * CHUNK : (first + count) * CHUNK]
 
-        z2_area = sb("z2_area", [P, 12 * CHUNK], F32)
-
-        def area(first, count, planes):
-            return z2_area[:, first * CHUNK : (first + count) * CHUNK].rearrange("p (t n) -> p t n", t=planes)
-
-        sig_first = [sb("sig_first1", [P, HALF], F32)[:], z2_area[:, cols(0, HALF)], z2_area[:, cols(1, HALF)]]
-        y_row3 = y_rows[:, 3].rearrange("p u c n -> p (u c n)")
-        sig_late = [y_row3[:, cols(t, HALF)] for t in range(2)] + [sb("sig_late3", [P, HALF], F32)]
-        z2_first = area(4, 8, PACK)
-        z2_planes = [z2_first, None, area(0, 8, PACK)[:, :, CHUNK:], area(8, 4, PACK)]
-        z2_spans = [halves[0], None, cols(2, CHUNK), cols(3, CHUNK)]
-
-        def picks(span):
-            return nb_t[:, span.start // LIST_ROWS : span.stop // LIST_ROWS]
+        z2_planes = [part(first, 8).rearrange("p (t n) -> p t n", t=PACK) for first in (4, 0)]
+        sig_first = [sb("sig_first1", [P, HALF], F32)[:], part(1, 2), sb("sig_first3", [P, HALF], F32)[:]]
+        y_row3 = y_rows[:, 2].rearrange("p u c n -> p (u c n)")
+        sig_late = [y_row3[:, halves[0]], y_row3[:, halves[1]], sb("sig_late3", [P, HALF], F32)[:]]
 
         def fetch_sigmoid(dst, t, span):
-            nc.scalar.activation(dst, windows[t][:].indirect(picks(span)), ACT.Sigmoid, scale=2.0)
-
-        def fetch_plane0(dst, span):
-            nc.vector.tensor_tensor(
-                dst, windows[0][:].indirect(picks(span)), gain_row[:, : span.stop - span.start], ALU.mult
-            )
-
-        def shift_and_gain(dst, src, t):
-            nc.vector.tensor_scalar(dst, src, 0.5, gain[:, t : t + 1], ALU.subtract, ALU.mult)
+            nc.scalar.activation(dst, windows[t][:].indirect(picks(nb_t, span)), ACT.Sigmoid, scale=2.0)
 
         for t in range(1, PACK):
             fetch_sigmoid(sig_first[t - 1], t, halves[0])
-
-        def scalar_shift_and_gain(dst, src, t):
-            nc.scalar.activation(
-                dst, src, ACT.Identity, bias=neg_half_gain[:, t : t + 1], scale=gain[:, t : t + 1]
-            )
-
         for t in range(1, 3):
             fetch_sigmoid(sig_late[t - 1], t, halves[1])
-        fetch_sigmoid(sig_late[2][:, cols(0, CHUNK)], 3, cols(2, CHUNK))
-        fetch_sigmoid(sig_late[2][:, cols(1, CHUNK)], 3, cols(3, CHUNK))
+        for i in range(2):
+            fetch_sigmoid(sig_late[2][:, cols(i, CHUNK)], 3, cols(2 + i, CHUNK))
+        for t in range(1, 3):
+            nc.gpsimd.tensor_scalar(
+                z2_planes[0][:, t, :], sig_first[t - 1], -0.5, gain[:, t : t + 1], ALU.add, ALU.mult
+            )
 
-        z2_bf = {}
+        z2q = (sb("z2_codes", [P, S], U32), sb("z2_scales", [P, S], U8))
+        late_words = sb("late_words", [P, 2 * HALF], F32)
+        z2_bf = [
+            sb("z2_bf_first", [P, HALF, PACK], BF16)[:],
+            late_words[:].bitcast(BF16).rearrange("p (n t) -> p n t", t=PACK),
+        ]
 
-        def weave_z2(c):
-            z2_bf[c] = sb("z2_bf%d" % c, [P, z2_spans[c].stop - z2_spans[c].start, PACK], BF16)
+        def fetch_plane0(dst, span):
+            nc.vector.tensor_copy(dst, windows[0][:].indirect(picks(nb_t, span)))
+
+        def weave_z2(u, span):
             nc.vector.tensor_copy(
-                out=z2_bf[c][:].rearrange("p (a i) t -> p a t i", i=RUN),
-                in_=z2_planes[c].rearrange("p t (a i) -> p a t i", i=RUN),
+                out=z2_bf[u][:, span, :].rearrange("p (a i) t -> p a t i", i=RUN),
+                in_=z2_planes[u][:, :, span].rearrange("p t (a i) -> p a t i", i=RUN),
             )
 
         def quantize_z2(c):
-            span = cols(c, CHUNK)
-            woven = z2_bf[0][:, span, :] if c < 2 else z2_bf[c][:]
-            nc.vector.quantize_mx(
-                out=z2_codes[:, span].bitcast(FP8X4),
-                scales=z2_scales[:, span],
-                in_=woven.rearrange("p n t -> p (n t)"),
-            )
+            quantize(z2q, cols(c, CHUNK), z2_bf[c // 2][:, cols(c % 2, CHUNK), :].rearrange("p n t -> p (n t)"))
 
-        def finish_added(t):
-            bank = psum.tile([P, HALF], F32, name=("chunk_bank%d" if t < 2 else "plane_bank%d") % (t % 2))
-            if t == 0:
-                for c in range(2):
-                    mx(bank[:, cols(c, CHUNK)], w2_codes, w2_scales, t, z2_codes, z2_scales, cols(2 + c, CHUNK), True, True)
+        def shift(dst, src, t):
+            nc.vector.tensor_scalar(dst, src, 0.5, gain[:, t : t + 1], ALU.subtract, ALU.mult)
+
+        out_rows = out.rearrange("(p t) n -> p t n", t=PACK)
+        added = {
+            (0, 1): bank("u_first1", [P, HALF], "bank3")[:],
+            (1, 1): bank("u_late1", [P, HALF], "bank4")[:],
+            (1, 2): bank("u_late2", [P, HALF], "bank0")[:],
+            (1, 3): bank("u_late3", [P, HALF], "bank1")[:],
+        }
+
+        def third_product(c, planes):
+            u, i = divmod(c, 2)
+            for t in planes:
+                if (u, t) in remade:
+                    mx(remade[u, t][:, cols(i, CHUNK)], w2q, t, z2q, cols(c, CHUNK), False, i == 1 and (u, t) != (0, 0))
+                else:
+                    mx(added[u, t][:, cols(i, CHUNK)], w2q, t, z2q, cols(c, CHUNK), True, True)
+
+        def finish(u, t):
+            res = sb("res%d_%d" % (u, t), [P, HALF], F32)
+            if (u, t) in remade:
+                nc.scalar.activation(res[:], remade[u, t], ACT.Tanh)
             else:
-                mx(bank[:], w2_codes, w2_scales, t, z2_codes, z2_scales, halves[1], True, True)
-            pre = sb("pre%d" % t, [P, HALF], F32)
-            nc.vector.tensor_tensor(pre[:], bank[:], y_sb[:, t, 1].rearrange("p c n -> p (c n)"), ALU.add)
-            nc.scalar.activation(res[1][:, t, :], pre[:], ACT.Tanh)
-            nc.sync.dma_start(out=out_rows[:, t, halves[1]], in_=res[1][:, t, :])
+                pre = late_words[:, halves[0]] if u == 0 else sb("pre%d" % t, [P, HALF], F32)[:]
+                nc.vector.tensor_tensor(pre, added[u, t], y_sb[:, t - 1, u].rearrange("p c n -> p (c n)"), ALU.add)
+                nc.scalar.activation(res[:], pre, ACT.Tanh)
+            nc.sync.dma_start(out=out_rows[:, t, halves[u]], in_=res[:])
 
-        fetch_plane0(z2_first[:, 0, :], halves[0])
+        fetch_plane0(z2_planes[0][:, 0, :], halves[0])
+        fetch_plane0(z2_planes[1][:, 0, cols(0, CHUNK)], cols(2, CHUNK))
+        shift(z2_planes[0][:, 3, :], sig_first[2], 3)
+        fetch_plane0(z2_planes[1][:, 0, cols(1, CHUNK)], cols(3, CHUNK))
+        weave_z2(0, slice(0, HALF))
+        for t in range(1, 3):
+            shift(z2_planes[1][:, t, cols(0, CHUNK)], sig_late[t - 1][:, cols(0, CHUNK)], t)
+        quantize_z2(0)
+        third_product(0, (3, 0, 2, 1))
+        shift(z2_planes[1][:, 3, cols(0, CHUNK)], sig_late[2][:, cols(0, CHUNK)], 3)
+        quantize_z2(1)
+        third_product(1, (3, 0, 2, 1))
         for t in range(1, PACK):
-            shift_and_gain(z2_first[:, t, :], sig_first[t - 1], t)
-        fetch_plane0(z2_planes[2][:, 0, :], cols(2, CHUNK))
-        weave_z2(0)
-        shift_and_gain(z2_planes[2][:, 1, :], sig_late[0][:, cols(0, CHUNK)], 1)
-        for c in range(2):
+            nc.scalar.activation(
+                z2_planes[1][:, t, cols(1, CHUNK)],
+                sig_late[t - 1][:, cols(1, CHUNK)],
+                ACT.Identity,
+                bias=neg_half_gain[:, t : t + 1],
+                scale=gain[:, t : t + 1],
+            )
+        for t in (3, 0, 2):
+            finish(0, t)
+        for i in range(2):
+            weave_z2(1, cols(i, CHUNK))
+        for c in range(2, CHUNKS):
             quantize_z2(c)
-            span = cols(c, CHUNK)
-            for t in range(2):
-                mx(first_banks[t][:, span], w2_codes, w2_scales, t, z2_codes, z2_scales, span, False, c == 1 and t == 1)
-        for t in range(2, PACK):
-            mx(first_banks[t], w2_codes, w2_scales, t, z2_codes, z2_scales, halves[0], False, t == 3)
-        for t in range(2, PACK):
-            shift_and_gain(z2_planes[2][:, t, :], sig_late[t - 1][:, cols(0, CHUNK)], t)
-        fetch_plane0(z2_planes[3][:, 0, :], cols(3, CHUNK))
-        weave_z2(2)
-        quantize_z2(2)
-        for t in range(1, PACK):
-            scalar_shift_and_gain(z2_planes[3][:, t, :], sig_late[t - 1][:, cols(1, CHUNK)], t)
+            third_product(c, (0, 1))
+        for t in (2, 3):
+            mx(added[1, t], w2q, t, z2q, halves[1], True, True)
+        finish(0, 1)
         for t in range(PACK):
-            nc.scalar.activation(res[0][:, t, :], first_banks[t], ACT.Tanh)
-            nc.sync.dma_start(out=out_rows[:, t, halves[0]], in_=res[0][:, t, :])
-        weave_z2(3)
-        quantize_z2(3)
-        for t in range(PACK):
-            finish_added(t)
+            finish(1, t)

@@ -23,7 +23,7 @@ HALF = S // 2
 QUADRANT = 32
 LIST_ROWS = 16
 RUN = 4
-W1_SCALAR = 72
+W1_SCALAR = 48
 
 
 def tile_picked_implicit2_none_p_kernel(
@@ -74,10 +74,12 @@ def tile_picked_implicit2_none_p_kernel(
         gain = sb("gain", [P, PACK], F32)
 
         nc.gpsimd.memset(xs[:].bitcast(I32), 0)
-        nc.sync.dma_start(out=w1_raw[:], in_=w1.rearrange("(p j) c -> p j c", j=PACK))
+        w1_rows = w1.rearrange("(p j) c -> p j c", j=PACK)
+        nc.sync.dma_start(out=w1_raw[:, 0:2, :], in_=w1_rows[:, 0:2, :])
         nc.sync.dma_start(offs_t[:], offs)
         for r in range(4):
             nc.sync.dma_start(out=xs[r:P:QUADRANT, :].bitcast(I32), in_=x_scales[0, r:16:4, :].bitcast(I32))
+        nc.sync.dma_start(out=w1_raw[:, 2:4, :], in_=w1_rows[:, 2:4, :])
         nc.sync.dma_start(out=xw[:].bitcast(I32), in_=x_words[0].rearrange("p n r -> p (n r)").bitcast(I32))
         w2_rows = w2.rearrange("(p j) c -> p j c", j=PACK)
         nc.sync.dma_start(out=w2_raw[0][:], in_=w2_rows[:, :, w2_parts[0]])
@@ -98,7 +100,9 @@ def tile_picked_implicit2_none_p_kernel(
             )
 
         w1_grouped = sb("w1_grouped", [P, PACK, P, PACK], BF16)
-        nc.scalar.copy(*weave_views(w1_grouped, w1_raw, slice(0, W1_SCALAR), slice(0, W1_SCALAR)))
+        dst, src = weave_views(w1_grouped, w1_raw, slice(0, W1_SCALAR), slice(0, W1_SCALAR))
+        for rows in (slice(0, 2), slice(2, 4)):
+            nc.scalar.copy(dst[:, :, rows], src[:, :, rows])
         nc.vector.tensor_copy(*weave_views(w1_grouped, w1_raw, slice(W1_SCALAR, P), slice(W1_SCALAR, P)))
         w1q = (placed.tile([P, H], U32, name="w1_codes", offset=0, align_bytes=64), sb("w1_scales", [P, H], U8))
         quantize(w1q, slice(0, H), w1_grouped[:].rearrange("p t m j -> p (t m j)"))
@@ -166,20 +170,24 @@ def tile_picked_implicit2_none_p_kernel(
         for c in range(CHUNKS):
             nc.scalar.copy(out=y_sb[:, :, c // 2, c % 2, :], in_=y_banks[c][:, 1:PACK, :])
 
-        h_banks += [bank("h%d" % t, [P, S], "bank%d" % (t - 1)) for t in range(1, PACK)]
-        for span in halves:
-            mx(h_banks[1][:, span], w2q, 1, zq, span, True, True)
-        for span in halves:
-            mx(h_banks[0][:, span], w2q, 0, zq, span, False, span == halves[1])
+        h1 = [bank("h1_%d" % u, [P, HALF], "bank%d" % u) for u in range(2)]
+        h_banks += [None] + [bank("h%d" % t, [P, S], "bank%d" % t) for t in range(2, PACK)]
+        for u in range(2):
+            mx(h1[u][:], w2q, 1, zq, halves[u], True, True)
+            mx(h_banks[0][:, halves[u]], w2q, 0, zq, halves[u], False, u == 1)
         for t in range(2, PACK):
             mx(h_banks[t][:], w2q, t, zq, every, True, True)
         windows = [sb("window%d" % t, [P, S], F32) for t in range(PACK)]
-        h0 = sb("h0_sb", [P, S], F32)
-        nc.scalar.activation(h0[:], h_banks[0][:], ACT.Tanh)
-        neg_half_gain = sb("neg_half_gain", [P, PACK], F32, tag="w2_grouped")
-        nc.gpsimd.tensor_scalar(neg_half_gain[:], gain[:], -0.5, 1.0, ALU.mult, ALU.mult)
-        nc.gpsimd.tensor_scalar(windows[0][:], h0[:], gain[:, 0:1], 0.5, ALU.mult, ALU.mult)
-        for t in range(1, PACK):
+        nc.scalar.activation(windows[0][:], h_banks[0][:], ACT.Tanh)
+        gains = sb("gains", [P, HALF + PACK], F32, tag="w2_grouped")
+        gain_row, neg_half_gain = gains[:, :HALF], gains[:, HALF:]
+        nc.gpsimd.tensor_scalar(gain_row, gain[:, 0:1].to_broadcast([P, HALF]), 0.5, 1.0, ALU.mult, ALU.mult)
+        nc.gpsimd.tensor_scalar(neg_half_gain, gain[:], -0.5, 1.0, ALU.mult, ALU.mult)
+        for u in range(2):
+            nc.vector.tensor_tensor(
+                windows[1][:, halves[u]], h1[u][:], y_sb[:, 0, u].rearrange("p c n -> p (c n)"), ALU.add
+            )
+        for t in range(2, PACK):
             nc.vector.tensor_tensor(
                 windows[t][:].rearrange("p (u n) -> p u n", u=2),
                 h_banks[t][:].rearrange("p (u n) -> p u n", u=2),
@@ -193,7 +201,7 @@ def tile_picked_implicit2_none_p_kernel(
             return area[:, first * CHUNK : (first + count) * CHUNK]
 
         z2_planes = [part(first, 8).rearrange("p (t n) -> p t n", t=PACK) for first in (4, 0)]
-        sig_first = [sb("sig_first1", [P, HALF], F32)[:], part(1, 2), sb("sig_first3", [P, HALF], F32)[:]]
+        sig_first = [sb("sig_first1", [P, HALF], F32)[:], sb("sig_first2", [P, HALF], F32)[:], part(2, 2)]
         y_row3 = y_rows[:, 2].rearrange("p u c n -> p (u c n)")
         sig_late = [y_row3[:, halves[0]], y_row3[:, halves[1]], sb("sig_late3", [P, HALF], F32)[:]]
 
@@ -206,10 +214,6 @@ def tile_picked_implicit2_none_p_kernel(
             fetch_sigmoid(sig_late[t - 1], t, halves[1])
         for i in range(2):
             fetch_sigmoid(sig_late[2][:, cols(i, CHUNK)], 3, cols(2 + i, CHUNK))
-        for t in range(1, 3):
-            nc.gpsimd.tensor_scalar(
-                z2_planes[0][:, t, :], sig_first[t - 1], -0.5, gain[:, t : t + 1], ALU.add, ALU.mult
-            )
 
         z2q = (sb("z2_codes", [P, S], U32), sb("z2_scales", [P, S], U8))
         late_words = sb("late_words", [P, 2 * HALF], F32)
@@ -219,7 +223,9 @@ def tile_picked_implicit2_none_p_kernel(
         ]
 
         def fetch_plane0(dst, span):
-            nc.vector.tensor_copy(dst, windows[0][:].indirect(picks(nb_t, span)))
+            nc.vector.tensor_tensor(
+                dst, windows[0][:].indirect(picks(nb_t, span)), gain_row[:, : span.stop - span.start], ALU.mult
+            )
 
         def weave_z2(u, span):
             nc.vector.tensor_copy(
@@ -235,7 +241,7 @@ def tile_picked_implicit2_none_p_kernel(
 
         out_rows = out.rearrange("(p t) n -> p t n", t=PACK)
         added = {
-            (0, 1): bank("u_first1", [P, HALF], "bank3")[:],
+            (0, 1): bank("u_first1", [P, HALF], "bank2")[:],
             (1, 1): bank("u_late1", [P, HALF], "bank4")[:],
             (1, 2): bank("u_late2", [P, HALF], "bank0")[:],
             (1, 3): bank("u_late3", [P, HALF], "bank1")[:],
@@ -260,21 +266,22 @@ def tile_picked_implicit2_none_p_kernel(
             nc.sync.dma_start(out=out_rows[:, t, halves[u]], in_=res[:])
 
         fetch_plane0(z2_planes[0][:, 0, :], halves[0])
+        for t in range(1, 3):
+            shift(z2_planes[0][:, t, :], sig_first[t - 1], t)
         fetch_plane0(z2_planes[1][:, 0, cols(0, CHUNK)], cols(2, CHUNK))
         shift(z2_planes[0][:, 3, :], sig_first[2], 3)
         fetch_plane0(z2_planes[1][:, 0, cols(1, CHUNK)], cols(3, CHUNK))
         weave_z2(0, slice(0, HALF))
-        for t in range(1, 3):
-            shift(z2_planes[1][:, t, cols(0, CHUNK)], sig_late[t - 1][:, cols(0, CHUNK)], t)
+        shift(z2_planes[1][:, 1, :], sig_late[0], 1)
         quantize_z2(0)
         third_product(0, (3, 0, 2, 1))
-        shift(z2_planes[1][:, 3, cols(0, CHUNK)], sig_late[2][:, cols(0, CHUNK)], 3)
+        shift(z2_planes[1][:, 2, cols(0, CHUNK)], sig_late[1][:, cols(0, CHUNK)], 2)
         quantize_z2(1)
         third_product(1, (3, 0, 2, 1))
-        for t in range(1, PACK):
+        for t, i in ((3, 0), (2, 1), (3, 1)):
             nc.scalar.activation(
-                z2_planes[1][:, t, cols(1, CHUNK)],
-                sig_late[t - 1][:, cols(1, CHUNK)],
+                z2_planes[1][:, t, cols(i, CHUNK)],
+                sig_late[t - 1][:, cols(i, CHUNK)],
                 ACT.Identity,
                 bias=neg_half_gain[:, t : t + 1],
                 scale=gain[:, t : t + 1],

@@ -178,11 +178,9 @@ def tile_picked_implicit2_none_p_kernel(
         for t in range(2, PACK):
             mx(h_banks[t][:], w2q, t, zq, every, True, True)
         windows = [sb("window%d" % t, [P, S], F32) for t in range(PACK)]
-        nc.scalar.activation(windows[0][:], h_banks[0][:], ACT.Tanh)
-        gains = sb("gains", [P, HALF + PACK], F32, tag="w2_grouped")
-        gain_row, neg_half_gain = gains[:, :HALF], gains[:, HALF:]
-        nc.gpsimd.tensor_scalar(gain_row, gain[:, 0:1].to_broadcast([P, HALF]), 0.5, 1.0, ALU.mult, ALU.mult)
-        nc.gpsimd.tensor_scalar(neg_half_gain, gain[:], -0.5, 1.0, ALU.mult, ALU.mult)
+        h_plane0 = sb("h_plane0", [P, S], F32)
+        nc.scalar.activation(h_plane0[:], h_banks[0][:], ACT.Tanh)
+        nc.gpsimd.tensor_scalar(windows[0][:], h_plane0[:], gain[:, 0:1], 0.5, ALU.mult, ALU.mult)
         for u in range(2):
             nc.vector.tensor_tensor(
                 windows[1][:, halves[u]], h1[u][:], y_sb[:, 0, u].rearrange("p c n -> p (c n)"), ALU.add
@@ -195,13 +193,8 @@ def tile_picked_implicit2_none_p_kernel(
                 ALU.add,
             )
 
-        area = sb("area", [P, 12 * CHUNK], F32)
-
-        def part(first, count):
-            return area[:, first * CHUNK : (first + count) * CHUNK]
-
-        z2_planes = [part(first, 8).rearrange("p (t n) -> p t n", t=PACK) for first in (4, 0)]
-        sig_first = [sb("sig_first1", [P, HALF], F32)[:], sb("sig_first2", [P, HALF], F32)[:], part(2, 2)]
+        z2_planes = sb("z2_planes", [P, PACK, HALF], F32)
+        sig_first = [sb("sig_first%d" % t, [P, HALF], F32)[:] for t in range(1, PACK)]
         y_row3 = y_rows[:, 2].rearrange("p u c n -> p (u c n)")
         sig_late = [y_row3[:, halves[0]], y_row3[:, halves[1]], sb("sig_late3", [P, HALF], F32)[:]]
 
@@ -210,10 +203,8 @@ def tile_picked_implicit2_none_p_kernel(
 
         for t in range(1, PACK):
             fetch_sigmoid(sig_first[t - 1], t, halves[0])
-        for t in range(1, 3):
+        for t in range(1, PACK):
             fetch_sigmoid(sig_late[t - 1], t, halves[1])
-        for i in range(2):
-            fetch_sigmoid(sig_late[2][:, cols(i, CHUNK)], 3, cols(2 + i, CHUNK))
 
         z2q = (sb("z2_codes", [P, S], U32), sb("z2_scales", [P, S], U8))
         late_words = sb("late_words", [P, 2 * HALF], F32)
@@ -222,15 +213,10 @@ def tile_picked_implicit2_none_p_kernel(
             late_words[:].bitcast(BF16).rearrange("p (n t) -> p n t", t=PACK),
         ]
 
-        def fetch_plane0(dst, span):
-            nc.vector.tensor_tensor(
-                dst, windows[0][:].indirect(picks(nb_t, span)), gain_row[:, : span.stop - span.start], ALU.mult
-            )
-
         def weave_z2(u, span):
             nc.vector.tensor_copy(
                 out=z2_bf[u][:, span, :].rearrange("p (a i) t -> p a t i", i=RUN),
-                in_=z2_planes[u][:, :, span].rearrange("p t (a i) -> p a t i", i=RUN),
+                in_=z2_planes[:, :, span].rearrange("p t (a i) -> p a t i", i=RUN),
             )
 
         def quantize_z2(c):
@@ -265,27 +251,20 @@ def tile_picked_implicit2_none_p_kernel(
                 nc.scalar.activation(res[:], pre, ACT.Tanh)
             nc.sync.dma_start(out=out_rows[:, t, halves[u]], in_=res[:])
 
-        fetch_plane0(z2_planes[0][:, 0, :], halves[0])
-        for t in range(1, 3):
-            shift(z2_planes[0][:, t, :], sig_first[t - 1], t)
-        fetch_plane0(z2_planes[1][:, 0, cols(0, CHUNK)], cols(2, CHUNK))
-        shift(z2_planes[0][:, 3, :], sig_first[2], 3)
-        fetch_plane0(z2_planes[1][:, 0, cols(1, CHUNK)], cols(3, CHUNK))
-        weave_z2(0, slice(0, HALF))
-        shift(z2_planes[1][:, 1, :], sig_late[0], 1)
-        quantize_z2(0)
-        third_product(0, (3, 0, 2, 1))
-        shift(z2_planes[1][:, 2, cols(0, CHUNK)], sig_late[1][:, cols(0, CHUNK)], 2)
-        quantize_z2(1)
-        third_product(1, (3, 0, 2, 1))
-        for t, i in ((3, 0), (2, 1), (3, 1)):
+        nc.vector.tensor_copy(z2_planes[:, 0, :], windows[0][:].indirect(picks(nb_t, halves[0])))
+        for t in range(1, PACK):
+            shift(z2_planes[:, t, :], sig_first[t - 1], t)
+        for i in range(2):
+            weave_z2(0, cols(i, CHUNK))
+        for c in range(2):
+            quantize_z2(c)
+            third_product(c, (3, 0, 2, 1))
+        for i in range(2):
             nc.scalar.activation(
-                z2_planes[1][:, t, cols(i, CHUNK)],
-                sig_late[t - 1][:, cols(i, CHUNK)],
-                ACT.Identity,
-                bias=neg_half_gain[:, t : t + 1],
-                scale=gain[:, t : t + 1],
+                z2_planes[:, 0, cols(i, CHUNK)], windows[0][:].indirect(picks(nb_t, cols(2 + i, CHUNK))), ACT.Copy
             )
+        for t in range(1, PACK):
+            shift(z2_planes[:, t, :], sig_late[t - 1], t)
         for t in (3, 0, 2):
             finish(0, t)
         for i in range(2):

from contextlib import ExitStack

import concourse.mybir as mybir

K, T, S, H = 512, 2048, 512, 512
FLOPS = 2 * S * H * (K + 2 * H)

F32 = mybir.dt.float32
BF16 = mybir.dt.bfloat16
I32 = mybir.dt.int32
U32 = mybir.dt.uint32
U16 = mybir.dt.uint16
U8 = mybir.dt.uint8
FP8X4 = mybir.dt.float8_e4m3fn_x4
ACT = mybir.ActivationFunctionType
ALU = mybir.AluOpType

P = 128
PACK = 4
CHUNK = 128
CHUNKS = S // CHUNK
HALF = S // 2
QUADRANT = 32
LIST_ROWS = 16
RUN = 4
W1_SCALAR = 48


def tile_picked_implicit2_none_p_kernel(
    tc, x_words, x_scales, w1, gn, w2, offs, nb, out
):
    nc = tc.nc
    with ExitStack() as ctx:
        keep = ctx.enter_context(tc.tile_pool(name="keep", bufs=1))
        placed = ctx.enter_context(tc.tile_pool(name="placed", bufs=1))
        psum = ctx.enter_context(tc.psum_pool(name="psum", bufs=1))

        def sb(name, shape, dtype, tag=None):
            return keep.tile(shape, dtype, name=name, tag=tag or name, align_bytes=64)

        def bank(name, shape, tag):
            return psum.tile(shape, F32, name=name, tag=tag)

        def cols(i, width):
            return slice(i * width, (i + 1) * width)

        def picks(lists, span):
            return lists[:, span.start // LIST_ROWS : span.stop // LIST_ROWS]

        def mx(dst, weight, t, nodes, span, start, stop):
            nc.tensor.matmul_mx(
                out=dst,
                lhsT=weight[0][:, cols(t, P)].bitcast(FP8X4),
                lhsT_scale=weight[1][:, cols(t, P)],
                rhs=nodes[0][:, span].bitcast(FP8X4),
                rhs_scale=nodes[1][:, span],
                start=start,
                stop=stop,
            )

        def quantize(dst, span, woven):
            nc.vector.quantize_mx(out=dst[0][:, span].bitcast(FP8X4), scales=dst[1][:, span], in_=woven)

        halves = [cols(u, HALF) for u in range(2)]
        every = slice(0, S)

        offs_t = keep.tile([P, S // LIST_ROWS], U16, name="offs_t")
        nb_t = keep.tile([P, S // LIST_ROWS], U16, name="nb_t")
        w1_raw = sb("w1_raw", [P, PACK, H], F32)
        w2_parts = [slice(0, H // 2), slice(H // 2, 3 * H // 4), slice(3 * H // 4, H)]
        w2_raw = [sb("w2_raw%d" % u, [P, PACK, part.stop - part.start], F32) for u, part in enumerate(w2_parts)]
        xw = sb("xw", [P, T], U32)
        xs = placed.tile([P, T], U8, name="xs", offset=T // 2, align_bytes=64)
        gain = sb("gain", [P, PACK], F32)

        nc.gpsimd.memset(xs[:].bitcast(I32), 0)
        w1_rows = w1.rearrange("(p j) c -> p j c", j=PACK)
        nc.sync.dma_start(out=w1_raw[:, 0:2, :], in_=w1_rows[:, 0:2, :])
        nc.sync.dma_start(offs_t[:], offs)
        for r in range(4):
            nc.sync.dma_start(out=xs[r:P:QUADRANT, :].bitcast(I32), in_=x_scales[0, r:16:4, :].bitcast(I32))
        nc.sync.dma_start(out=w1_raw[:, 2:4, :], in_=w1_rows[:, 2:4, :])
        nc.sync.dma_start(out=xw[:].bitcast(I32), in_=x_words[0].rearrange("p n r -> p (n r)").bitcast(I32))
        w2_rows = w2.rearrange("(p j) c -> p j c", j=PACK)
        nc.sync.dma_start(out=w2_raw[0][:], in_=w2_rows[:, :, w2_parts[0]])
        nc.sync.dma_start(out=w2_raw[1][:], in_=w2_rows[:, :, w2_parts[1]])
        nc.sync.dma_start(out=gain[:], in_=gn.rearrange("(p t) o -> p (t o)", t=PACK))
        nc.sync.dma_start(out=w2_raw[2][:], in_=w2_rows[:, :, w2_parts[2]])
        nc.sync.dma_start(nb_t[:], nb)

        xq_scales = sb("xq_scales", [P, S], U8)
        nc.vector.tensor_copy(xq_scales[:], xs[:].indirect(offs_t[:]))

        def weave_views(grouped, raw, m_dst, m_src):
            return (
                grouped[:, :, m_dst, :].rearrange("p t (a b) j -> p a j t b", b=2),
                raw[:].rearrange("p j (m t) -> p j m t", t=PACK)[:, :, m_src, :].rearrange(
                    "p j (a b) t -> p a j t b", b=2
                ),
            )

        w1_grouped = sb("w1_grouped", [P, PACK, P, PACK], BF16)
        dst, src = weave_views(w1_grouped, w1_raw, slice(0, W1_SCALAR), slice(0, W1_SCALAR))
        for rows in (slice(0, 2), slice(2, 4)):
            nc.scalar.copy(dst[:, :, rows], src[:, :, rows])
        nc.vector.tensor_copy(*weave_views(w1_grouped, w1_raw, slice(W1_SCALAR, P), slice(W1_SCALAR, P)))
        w1q = (placed.tile([P, H], U32, name="w1_codes", offset=0, align_bytes=64), sb("w1_scales", [P, H], U8))
        quantize(w1q, slice(0, H), w1_grouped[:].rearrange("p t m j -> p (t m j)"))

        xq = (placed.tile([P, S], U32, name="xq_codes", offset=4 * H, align_bytes=64), xq_scales)
        for span in [cols(0, CHUNK), cols(1, CHUNK), halves[1]]:
            nc.vector.tensor_copy(xq[0][:, span], xw[:].indirect(picks(offs_t, span)))

        w2_grouped = sb("w2_grouped", [P, PACK, P, PACK], BF16)
        nc.vector.tensor_copy(*weave_views(w2_grouped, w2_raw[0], slice(0, P // 2), slice(0, P // 2)))
        nc.vector.tensor_copy(*weave_views(w2_grouped, w2_raw[1], slice(P // 2, 3 * P // 4), slice(0, P // 4)))

        y_banks = []
        sig_y = []
        for c in range(CHUNKS):
            y_banks.append(bank("y%d" % c, [P, PACK, CHUNK], "bank%d" % c))
            for t in range(PACK):
                mx(y_banks[c][:, t, :], w1q, t, xq, cols(c, CHUNK), True, True)
            sig_y.append(sb("sig_y%d" % c, [P, CHUNK, PACK], F32))
            nc.scalar.activation(sig_y[c][:], y_banks[c][:].rearrange("p t n -> p n t"), ACT.Sigmoid, scale=2.0)
        nc.scalar.copy(*weave_views(w2_grouped, w2_raw[2], slice(3 * P // 4, P), slice(0, P // 4)))

        h_banks = [bank("h0", [P, S], "bank4")]
        mx(h_banks[0][:], w1q, 0, xq, every, True, False)
        pair = bank("out_pair", [P, 2, HALF], "bank5")
        remade = {
            (0, 3): bank("out_first3", [P, HALF], "bank6")[:],
            (0, 0): pair[:, 0, :],
            (0, 2): pair[:, 1, :],
            (1, 0): bank("out_late0", [P, HALF], "bank7")[:],
        }
        for (u, t), dst in remade.items():
            mx(dst, w1q, t, xq, halves[u], (u, t) != (0, 2), False)

        zq = (sb("z_codes", [P, S], U32), sb("z_scales", [P, S], U8))
        w2q = (sb("w2_codes", [P, H], U32), sb("w2_scales", [P, H], U8))
        z_bf = sb("z_bf", [P, S, PACK], BF16)

        def make_z(c):
            nc.vector.scalar_tensor_tensor(
                z_bf[:, cols(c, CHUNK), :],
                sig_y[c][:],
                0.5,
                gain[:].unsqueeze(1).to_broadcast([P, CHUNK, PACK]),
                ALU.subtract,
                ALU.mult,
            )

        def quantize_z(u):
            quantize(zq, halves[u], z_bf[:, halves[u], :].rearrange("p n t -> p (n t)"))

        def quantize_w2(u):
            quantize(w2q, halves[u], w2_grouped[:, 2 * u : 2 * u + 2].rearrange("p t m j -> p (t m j)"))

        for c in range(3):
            make_z(c)
        quantize_z(0)
        make_z(3)
        quantize_w2(0)
        quantize_z(1)
        quantize_w2(1)

        y_rows = sb("y_rows", [P, PACK - 1, 2, 3, CHUNK], F32, tag="sig_y0")
        y_sb = y_rows[:, :, :, 1:3, :]
        for c in range(CHUNKS):
            nc.scalar.copy(out=y_sb[:, :, c // 2, c % 2, :], in_=y_banks[c][:, 1:PACK, :])

        h1 = [bank("h1_%d" % u, [P, HALF], "bank%d" % u) for u in range(2)]
        h_banks += [None] + [bank("h%d" % t, [P, S], "bank%d" % t) for t in range(2, PACK)]
        for u in range(2):
            mx(h1[u][:], w2q, 1, zq, halves[u], True, True)
            mx(h_banks[0][:, halves[u]], w2q, 0, zq, halves[u], False, u == 1)
        for t in range(2, PACK):
            mx(h_banks[t][:], w2q, t, zq, every, True, True)
        windows = [sb("window%d" % t, [P, S], F32) for t in range(PACK)]
        h_plane0 = sb("h_plane0", [P, S], F32)
        nc.scalar.activation(h_plane0[:], h_banks[0][:], ACT.Tanh)
        nc.gpsimd.tensor_scalar(windows[0][:], h_plane0[:], gain[:, 0:1], 0.5, ALU.mult, ALU.mult)
        for u in range(2):
            nc.vector.tensor_tensor(
                windows[1][:, halves[u]], h1[u][:], y_sb[:, 0, u].rearrange("p c n -> p (c n)"), ALU.add
            )
        for t in range(2, PACK):
            nc.vector.tensor_tensor(
                windows[t][:].rearrange("p (u n) -> p u n", u=2),
                h_banks[t][:].rearrange("p (u n) -> p u n", u=2),
                y_sb[:, t - 1].rearrange("p u c n -> p u (c n)"),
                ALU.add,
            )

        z2_planes = sb("z2_planes", [P, PACK, HALF], F32)
        sig_first = [sb("sig_first%d" % t, [P, HALF], F32)[:] for t in range(1, PACK)]
        y_row3 = y_rows[:, 2].rearrange("p u c n -> p (u c n)")
        sig_late = [y_row3[:, halves[0]], y_row3[:, halves[1]], sb("sig_late3", [P, HALF], F32)[:]]

        def fetch_sigmoid(dst, t, span):
            nc.scalar.activation(dst, windows[t][:].indirect(picks(nb_t, span)), ACT.Sigmoid, scale=2.0)

        for t in range(1, PACK):
            fetch_sigmoid(sig_first[t - 1], t, halves[0])
        for t in range(1, PACK):
            fetch_sigmoid(sig_late[t - 1], t, halves[1])

        z2q = (sb("z2_codes", [P, S], U32), sb("z2_scales", [P, S], U8))
        late_words = sb("late_words", [P, 2 * HALF], F32)
        z2_bf = [
            sb("z2_bf_first", [P, HALF, PACK], BF16)[:],
            late_words[:].bitcast(BF16).rearrange("p (n t) -> p n t", t=PACK),
        ]

        def weave_z2(u, span):
            nc.vector.tensor_copy(
                out=z2_bf[u][:, span, :].rearrange("p (a i) t -> p a t i", i=RUN),
                in_=z2_planes[:, :, span].rearrange("p t (a i) -> p a t i", i=RUN),
            )

        def quantize_z2(c):
            quantize(z2q, cols(c, CHUNK), z2_bf[c // 2][:, cols(c % 2, CHUNK), :].rearrange("p n t -> p (n t)"))

        def shift(dst, src, t):
            nc.vector.tensor_scalar(dst, src, 0.5, gain[:, t : t + 1], ALU.subtract, ALU.mult)

        out_rows = out.rearrange("(p t) n -> p t n", t=PACK)
        added = {
            (0, 1): bank("u_first1", [P, HALF], "bank2")[:],
            (1, 1): bank("u_late1", [P, HALF], "bank4")[:],
            (1, 2): bank("u_late2", [P, HALF], "bank0")[:],
            (1, 3): bank("u_late3", [P, HALF], "bank1")[:],
        }

        def third_product(c, planes):
            u, i = divmod(c, 2)
            for t in planes:
                if (u, t) in remade:
                    mx(remade[u, t][:, cols(i, CHUNK)], w2q, t, z2q, cols(c, CHUNK), False, i == 1 and (u, t) != (0, 0))
                else:
                    mx(added[u, t][:, cols(i, CHUNK)], w2q, t, z2q, cols(c, CHUNK), True, True)

        def finish(u, t):
            res = sb("res%d_%d" % (u, t), [P, HALF], F32)
            if (u, t) in remade:
                nc.scalar.activation(res[:], remade[u, t], ACT.Tanh)
            else:
                pre = late_words[:, halves[0]] if u == 0 else sb("pre%d" % t, [P, HALF], F32)[:]
                nc.vector.tensor_tensor(pre, added[u, t], y_sb[:, t - 1, u].rearrange("p c n -> p (c n)"), ALU.add)
                nc.scalar.activation(res[:], pre, ACT.Tanh)
            nc.sync.dma_start(out=out_rows[:, t, halves[u]], in_=res[:])

        nc.vector.tensor_copy(z2_planes[:, 0, :], windows[0][:].indirect(picks(nb_t, halves[0])))
        for t in range(1, PACK):
            shift(z2_planes[:, t, :], sig_first[t - 1], t)
        for i in range(2):
            weave_z2(0, cols(i, CHUNK))
        for c in range(2):
            quantize_z2(c)
            third_product(c, (3, 0, 2, 1))
        for i in range(2):
            nc.scalar.activation(
                z2_planes[:, 0, cols(i, CHUNK)], windows[0][:].indirect(picks(nb_t, cols(2 + i, CHUNK))), ACT.Copy
            )
        for t in range(1, PACK):
            shift(z2_planes[:, t, :], sig_late[t - 1], t)
        for t in (3, 0, 2):
            finish(0, t)
        for i in range(2):
            weave_z2(1, cols(i, CHUNK))
        for c in range(2, CHUNKS):
            quantize_z2(c)
            third_product(c, (0, 1))
        for t in (2, 3):
            mx(added[1, t], w2q, t, z2q, halves[1], True, True)
        finish(0, 1)
        for t in range(PACK):
            finish(1, t)
